import numpy as np
import ml_dtypes


def mxq(x, axis, fmt="e4m3"):
    dtype, down = {"e4m3": (ml_dtypes.float8_e4m3fn, 7), "e5m2": (ml_dtypes.float8_e5m2, 14)}[fmt]
    v = np.moveaxis(np.asarray(x, np.float32).astype(ml_dtypes.bfloat16).astype(np.float64), axis, -1)
    blocks = v.reshape(v.shape[:-1] + (-1, 32))
    amax = np.abs(blocks).max(-1, keepdims=True)
    byte = np.maximum(np.where(amax > 0, np.frexp(amax)[1] - 1 + 127, 0) - down, 1)
    scale = np.exp2(byte - 127.0)
    codes = (blocks / scale).astype(np.float32).astype(dtype).astype(np.float64)
    return np.moveaxis((codes * scale).reshape(v.shape), -1, axis)


WIDE = False


def mx_kscale(k):
    if not WIDE:
        return np.ones(k)
    levels = np.array([10, -10, 5, -5, 0])
    if k % 512:
        return np.exp2(np.random.permutation(np.resize(levels, k // 32))).repeat(32)
    a = np.empty((k // 512, 16))
    for p in range(k // 512):
        a[p, :8] = np.random.permutation(np.resize(levels, 8))
        for g in range(8):
            far = levels[np.abs(levels - a[p, g]) >= 10]
            a[p, g + 8] = far[np.random.randint(len(far))]
    return np.exp2(a.ravel()).repeat(32)


def f64(x):
    return np.asarray(x).astype(np.float64)


def striped(idx):
    return np.tile(idx.reshape(-1, 16).T, (8, 1)).astype(np.uint16)


def unstriped(offs):
    return offs[:16].T.reshape(-1).astype(np.int64)


E2M1 = np.array([0.0, 0.5, 1.0, 1.5, 2.0, 3.0, 4.0, 6.0, -0.0, -0.5, -1.0, -1.5, -2.0, -3.0, -4.0, -6.0])


def pack_weight(w, fmt):
    k, n = w.shape
    w = f64(np.asarray(w, np.float32).astype(ml_dtypes.bfloat16)).reshape(k // 32, 32, n)
    amax = np.abs(w).max(1)
    if fmt == "e4m3":
        byte = np.frexp(amax)[1] - 1 + 127 - 7
    else:
        mant, ex = np.frexp(amax / 6.0)
        byte = np.where(mant > 0.5, ex, ex - 1) + 127
    byte = np.clip(np.where(amax > 0, byte, 1), 1, 254)
    scaled = (w * np.exp2(127.0 - byte)[:, None, :]).reshape(k, n).astype(np.float32)
    by_word = np.ascontiguousarray(scaled.reshape(k // 512, 128, 4, n).transpose(0, 1, 3, 2))
    if fmt == "e4m3":
        words = by_word.astype(ml_dtypes.float8_e4m3fn).view(np.uint8)
    else:
        c = by_word.astype(ml_dtypes.float4_e2m1fn).view(np.uint8) & 0xF
        words = (c[..., 0::2] | (c[..., 1::2] << 4)).reshape(k // 512, 128, 2 * n)
    return np.ascontiguousarray(words), np.ascontiguousarray(byte.astype(np.uint8).reshape(k // 512, 16, n))


def unpack_weight(words, scales, fmt):
    g, _, n = scales.shape
    words = np.ascontiguousarray(words).reshape(g, 128, n, -1)
    if fmt == "e4m3":
        vals = words.view(ml_dtypes.float8_e4m3fn).astype(np.float64)
    else:
        nib = np.empty((g, 128, n, 4), np.uint8)
        nib[..., 0::2] = words & 0xF
        nib[..., 1::2] = words >> 4
        vals = E2M1[nib]
    vals = vals * np.repeat(np.exp2(scales.astype(np.float64) - 127.0), 8, axis=1)[..., None]
    return vals.transpose(0, 1, 3, 2).reshape(g * 512, n)


def gelu(v):
    return 0.5 * v * (1.0 + np.tanh(np.sqrt(2.0 / np.pi) * (v + 0.044715 * v**3)))


K, R, N, T, S = 1024, 512, 1024, 2048, 1024

def setup_inputs():
    n = np.random.standard_normal
    s = mx_kscale(K)[:, None]
    u = mx_kscale(R)[:, None]
    tab_words, tab_scales = pack_weight(n((K, T)) * s, "e4m3")
    w4_words, w4_scales = pack_weight(n((K, N)) / np.sqrt(K) / s, "e2m1")
    return {
        "tab_words": tab_words, "tab_scales": tab_scales,
        "offs": striped(np.random.permutation(T)[:S]),
        "wa": (n((K, R)) / np.sqrt(K) / s * u.T).astype(np.float32),
        "ba": (0.5 * n(R) * u[:, 0]).astype(np.float32),
        "gT": (1.0 + 0.5 * n((R, T))).astype(np.float32),
        "wb": (n((R, N)) / np.sqrt(R) / u).astype(np.float32),
        "w4_words": w4_words, "w4_scales": w4_scales,
        "bo": (0.5 * n(N)).astype(np.float32),
    }

def reference(tab_words, tab_scales, offs, wa, ba, gT, wb, w4_words, w4_scales, bo):
    v = unpack_weight(tab_words, tab_scales, "e4m3")[:, unstriped(offs)]
    g = f64(gT)[:, unstriped(offs)]
    a = mxq(f64(wa), 0, "e4m3").T @ v
    h = (a + f64(ba)[:, None]) * g
    hq = mxq(h, 0, "e4m3")
    w4 = unpack_weight(w4_words, w4_scales, "e2m1")
    y = w4.T @ v + mxq(f64(wb), 0, "e4m3").T @ hq
    return y + f64(bo)[:, None]

@@ -1,0 +1,226 @@
+from contextlib import ExitStack
+
+import concourse.mybir as mybir
+from concourse.masks import make_identity
+
+K, R, N, T, S = 1024, 512, 1024, 2048, 1024
+FLOPS = 2 * S * (K * R + K * N + R * N)
+
+F32 = mybir.dt.float32
+BF16 = mybir.dt.bfloat16
+I32 = mybir.dt.int32
+U32 = mybir.dt.uint32
+U16 = mybir.dt.uint16
+U8 = mybir.dt.uint8
+FP8X4 = mybir.dt.float8_e4m3fn_x4
+FP4X4 = mybir.dt.float4_e2m1fn_x4
+IDENTITY = mybir.ActivationFunctionType.Identity
+MULT = mybir.AluOpType.mult
+
+P = 128
+PACK = 4
+K_PASS = P * PACK
+PASSES = K // K_PASS
+HALF = 512
+HALVES = S // HALF
+N_TILES = N // P
+WB_COLS = 256
+SHIFT_ROWS = 112
+
+
+def tile_list_tenant_rank_scales_kernel(
+    tc, tab_words, tab_scales, offs, wa, ba, gT, wb, w4_words, w4_scales, bo, out
+):
+    nc = tc.nc
+    with ExitStack() as ctx:
+        keep = ctx.enter_context(tc.tile_pool(name="keep", bufs=1))
+        psum = ctx.enter_context(tc.psum_pool(name="psum", bufs=1))
+
+        offsets = keep.tile([P, S // 16], U16, name="offsets")
+        nc.sync.dma_start(offsets[:], offs)
+
+        tab_planes = keep.tile([P, T], U8, name="tab_planes", align_bytes=64)
+        nc.vector.memset(tab_planes[:].bitcast(I32), 0)
+        ba_cols = keep.tile([P, PACK], F32, name="ba_cols")
+        bo_rows = keep.tile([P, P], F32, name="bo_rows")
+        nc.vector.memset(bo_rows[:], 0.0)
+        ident = keep.tile([P, P], F32, name="ident")
+        make_identity(nc, ident[:])
+        v_plane1 = keep.tile([P, S], U8, name="v_plane1", align_bytes=64)
+        nc.vector.memset(v_plane1[:].bitcast(I32), 0)
+        w4_planes = keep.tile([P, PASSES, N], U8, name="w4_planes", align_bytes=64)
+        nc.vector.memset(w4_planes[:].bitcast(I32), 0)
+
+        tab_win = []
+        for a in range(PASSES):
+            win = keep.tile([P, T], U32, name=f"tab_win{a}", align_bytes=64)
+            nc.sync.dma_start(
+                out=win[:].bitcast(I32),
+                in_=tab_words[a].rearrange("p t i -> p (t i)").bitcast(I32),
+            )
+            tab_win.append(win)
+            if a == 0:
+                for q in range(4):
+                    nc.sync.dma_start(
+                        out=tab_planes[32 * q : 32 * q + 8, :].bitcast(I32),
+                        in_=tab_scales[:, 4 * q : 4 * q + 4, :].bitcast(I32),
+                    )
+        wa_raw = []
+        for a in range(PASSES):
+            raw = keep.tile([P, PACK, R], F32, name=f"wa_raw{a}")
+            nc.sync.dma_start(
+                out=raw[:],
+                in_=wa[a * K_PASS : (a + 1) * K_PASS, :].rearrange("(p j) r -> p j r", j=PACK),
+            )
+            wa_raw.append(raw)
+        nc.sync.dma_start(out=ba_cols[:], in_=ba.rearrange("(p t) -> p t", t=PACK))
+        nc.sync.dma_start(out=bo_rows[0:N_TILES, :], in_=bo.rearrange("(c p) -> c p", p=P))
+        v_codes = [keep.tile([P, S], U32, name=f"v_codes{a}", align_bytes=64) for a in range(PASSES)]
+        v_planes = keep.tile([P, S], U8, name="v_planes", align_bytes=64)
+        nc.vector.tensor_copy(out=v_codes[0][:], in_=tab_win[0][:].indirect(offsets[:]))
+        nc.vector.tensor_copy(out=v_planes[:], in_=tab_planes[:].indirect(offsets[:]))
+        nc.vector.tensor_copy(out=v_codes[1][:], in_=tab_win[1][:].indirect(offsets[:]))
+        nc.sync.dma_start(
+            out=v_plane1[0:SHIFT_ROWS, :].bitcast(I32),
+            in_=v_planes[4 : 4 + SHIFT_ROWS, :].bitcast(I32),
+        )
+
+        g_win = []
+        g_rows = gT.rearrange("(p t) c -> t p c", t=PACK)
+        for t in range(PACK):
+            win = keep.tile([P, T], F32, name=f"g_win{t}", align_bytes=64)
+            nc.sync.dma_start(out=win[:], in_=g_rows[t])
+            g_win.append(win)
+        for q in range(4):
+            nc.sync.dma_start(
+                out=w4_planes[32 * q : 32 * q + 4, :, :].bitcast(I32),
+                in_=w4_scales[:, 4 * q : 4 * q + 4, :].rearrange("a r c -> r a c").bitcast(I32),
+            )
+        w4_codes = keep.tile([P, PASSES, 2 * N], U8, name="w4_codes", align_bytes=64)
+        nc.sync.dma_start(
+            out=w4_codes[:].bitcast(I32),
+            in_=w4_words.rearrange("a p c -> p a c").bitcast(I32),
+        )
+        wb_raw = []
+        wb_rows = wb.rearrange("(p j) n -> p j n", j=PACK)
+        for c in range(N // WB_COLS):
+            raw = keep.tile([P, PACK, WB_COLS], F32, name=f"wb_raw{c}")
+            nc.sync.dma_start(out=raw[:], in_=wb_rows[:, :, c * WB_COLS : (c + 1) * WB_COLS])
+            wb_raw.append(raw)
+
+        bo_bank = psum.tile([P, P], F32, name="bo_bank", tag="bank7")
+        nc.tensor.transpose(bo_bank[:], bo_rows[:], ident[:])
+        bo_cols = keep.tile([P, N_TILES], F32, name="bo_cols")
+        nc.scalar.activation(out=bo_cols[:], in_=bo_bank[:, 0:N_TILES], func=IDENTITY)
+
+        wa_codes, wa_planes = [], []
+        for a in range(PASSES):
+            woven = keep.tile([P, PACK * R], BF16, name=f"wa_woven{a}", align_bytes=64)
+            nc.scalar.copy(
+                out=woven[:].rearrange("p (t m j) -> p m j t", t=PACK, j=PACK),
+                in_=wa_raw[a][:].rearrange("p j (m t) -> p m j t", t=PACK),
+            )
+            codes = keep.tile([P, R], U32, name=f"wa_codes{a}", align_bytes=64)
+            plane = keep.tile([P, R], U8, name=f"wa_plane{a}", align_bytes=64)
+            nc.vector.quantize_mx(out=codes[:].bitcast(FP8X4), scales=plane[:], in_=woven[:])
+            wa_codes.append(codes)
+            wa_planes.append(plane)
+
+        a4 = [keep.tile([P, PACK * HALF], F32, name=f"a4_{h}")[:] for h in range(HALVES)]
+        g4 = [keep.tile([P, PACK * HALF], F32, name=f"g4_{h}", align_bytes=64)[:] for h in range(HALVES)]
+        h_woven = [keep.tile([P, PACK * HALF], BF16, name=f"h_woven{h}", align_bytes=64)[:] for h in range(HALVES)]
+        wb_woven = [
+            g4[1][:, (PACK - 1) * HALF :].bitcast(BF16),
+            h_woven[1][:, : PACK * WB_COLS],
+            keep.tile([P, PACK * WB_COLS], BF16, name="wb_woven2", align_bytes=64)[:],
+            keep.tile([P, PACK * WB_COLS], BF16, name="wb_woven3", align_bytes=64)[:],
+        ]
+        for h in range(HALVES):
+            cols = slice(h * HALF, (h + 1) * HALF)
+            for t in range(PACK):
+                bank = psum.tile([P, HALF], F32, name=f"a_bank{h}_{t}", tag=f"bank{PACK * h + t}")
+                for a in range(PASSES):
+                    nc.tensor.matmul_mx(
+                        out=bank[:],
+                        lhsT=wa_codes[a][:, t * P : (t + 1) * P].bitcast(FP8X4),
+                        lhsT_scale=wa_planes[a][:, t * P : (t + 1) * P],
+                        rhs=v_codes[a][:, cols].bitcast(FP8X4),
+                        rhs_scale=v_planes[4 * a : P, cols],
+                        start=(a == 0),
+                        stop=(a == PASSES - 1),
+                    )
+                nc.scalar.activation(
+                    out=a4[h][:, t * HALF : (t + 1) * HALF], in_=bank[:], func=IDENTITY, bias=ba_cols[:, t : t + 1]
+                )
+
+
+        def gather_g(h, t):
+            lists = offsets[:, h * (HALF // 16) : (h + 1) * (HALF // 16)]
+            nc.vector.tensor_copy(out=g4[h][:, t * HALF : (t + 1) * HALF], in_=g_win[t][:].indirect(lists))
+
+        def make_h(h):
+            woven = h_woven[h]
+            nc.vector.tensor_tensor(
+                out=woven[:].rearrange("p (c i t) -> p c t i", i=4, t=PACK),
+                in0=a4[h].rearrange("p (t c i) -> p c t i", t=PACK, i=4),
+                in1=g4[h].rearrange("p (t c i) -> p c t i", t=PACK, i=4),
+                op=MULT,
+            )
+            codes = keep.tile([P, HALF], U32, name=f"h_codes{h}", align_bytes=64)
+            plane = keep.tile([P, HALF], U8, name=f"h_plane{h}", align_bytes=64)
+            nc.vector.quantize_mx(out=codes[:].bitcast(FP8X4), scales=plane[:], in_=woven[:])
+            return codes, plane
+
+        def quantise_wb(c):
+            woven = wb_woven[c]
+            nc.scalar.copy(
+                out=woven[:].rearrange("p (c i j) -> p c j i", i=4, j=PACK),
+                in_=wb_raw[c][:].rearrange("p j (c i) -> p c j i", i=4),
+            )
+            codes = keep.tile([P, WB_COLS], U32, name=f"wb_codes{c}", align_bytes=64)
+            plane = keep.tile([P, WB_COLS], U8, name=f"wb_plane{c}", align_bytes=64)
+            nc.vector.quantize_mx(out=codes[:].bitcast(FP8X4), scales=plane[:], in_=woven[:])
+            return codes, plane
+
+        for t in range(PACK - 1):
+            for h in range(HALVES):
+                gather_g(h, t)
+        gather_g(0, PACK - 1)
+        h_mx = [make_h(0)]
+        wb_mx = [quantise_wb(c) for c in range(N // WB_COLS)]
+        gather_g(1, PACK - 1)
+        h_mx.append(make_h(1))
+
+        v_scales = [v_planes, v_plane1]
+        for h in range(HALVES):
+            cols = slice(h * HALF, (h + 1) * HALF)
+            for n in range(N_TILES):
+                bank = psum.tile([P, HALF], F32, name=f"y_bank{h}_{n}", tag=f"bank{n}")
+                for a in range(PASSES):
+                    nc.tensor.matmul_mx(
+                        out=bank[:],
+                        lhsT=w4_codes[:, a, 2 * n * P : 2 * (n + 1) * P].bitcast(FP4X4),
+                        lhsT_scale=w4_planes[:, a, n * P : (n + 1) * P],
+                        rhs=v_codes[a][:, cols].bitcast(FP8X4),
+                        rhs_scale=v_scales[a][:, cols],
+                        start=(a == 0),
+                        stop=False,
+                    )
+                c, m0 = divmod(n * P, WB_COLS)
+                nc.tensor.matmul_mx(
+                    out=bank[:],
+                    lhsT=wb_mx[c][0][:, m0 : m0 + P].bitcast(FP8X4),
+                    lhsT_scale=wb_mx[c][1][:, m0 : m0 + P],
+                    rhs=h_mx[h][0][:].bitcast(FP8X4),
+                    rhs_scale=h_mx[h][1][:],
+                    start=False,
+                    stop=True,
+                )
+                result = keep.tile([P, HALF], F32, name=f"result{h}_{n}")
+                if h == 1 and n % 2 == 0:
+                    nc.vector.tensor_scalar_add(out=result[:], in0=bank[:], scalar1=bo_cols[:, n : n + 1])
+                else:
+                    nc.scalar.activation(
+                        out=result[:], in_=bank[:], func=IDENTITY, bias=bo_cols[:, n : n + 1]
+                    )
+                nc.sync.dma_start(out=out[n * P : (n + 1) * P, cols], in_=result[:])

@@ -24,8 +24,10 @@ PASSES = K // K_PASS
 HALF = 512
 HALVES = S // HALF
 N_TILES = N // P
+WB_LOAD = 256
 WB_COLS = 256
 SHIFT_ROWS = 112
+AHEAD = 4
 
 
 def tile_list_tenant_rank_scales_kernel(
@@ -51,46 +53,51 @@ def tile_list_tenant_rank_scales_kernel(
         w4_planes = keep.tile([P, PASSES, N], U8, name="w4_planes", align_bytes=64)
         nc.vector.memset(w4_planes[:].bitcast(I32), 0)
 
-        tab_win = []
-        for a in range(PASSES):
+        def load_table(a):
             win = keep.tile([P, T], U32, name=f"tab_win{a}", align_bytes=64)
             nc.sync.dma_start(
                 out=win[:].bitcast(I32),
                 in_=tab_words[a].rearrange("p t i -> p (t i)").bitcast(I32),
             )
-            tab_win.append(win)
-            if a == 0:
-                for q in range(4):
-                    nc.sync.dma_start(
-                        out=tab_planes[32 * q : 32 * q + 8, :].bitcast(I32),
-                        in_=tab_scales[:, 4 * q : 4 * q + 4, :].bitcast(I32),
-                    )
-        wa_raw = []
-        for a in range(PASSES):
+            return win
+
+        def load_wa(a):
             raw = keep.tile([P, PACK, R], F32, name=f"wa_raw{a}")
             nc.sync.dma_start(
                 out=raw[:],
                 in_=wa[a * K_PASS : (a + 1) * K_PASS, :].rearrange("(p j) r -> p j r", j=PACK),
             )
-            wa_raw.append(raw)
-        nc.sync.dma_start(out=ba_cols[:], in_=ba.rearrange("(p t) -> p t", t=PACK))
+            return raw
+
+        g_rows = gT.rearrange("(p t) c -> t p c", t=PACK)
+
+        def load_g(t):
+            win = keep.tile([P, T], F32, name=f"g_win{t}", align_bytes=64)
+            nc.sync.dma_start(out=win[:], in_=g_rows[t])
+            return win
+
+        tab_win = [load_table(0)]
+        for q in range(4):
+            nc.sync.dma_start(
+                out=tab_planes[32 * q : 32 * q + 8, :].bitcast(I32),
+                in_=tab_scales[:, 4 * q : 4 * q + 4, :].bitcast(I32),
+            )
         nc.sync.dma_start(out=bo_rows[0:N_TILES, :], in_=bo.rearrange("(c p) -> c p", p=P))
+        wa_raw = [load_wa(a) for a in range(PASSES)]
+        tab_win.append(load_table(1))
+        nc.sync.dma_start(out=ba_cols[:], in_=ba.rearrange("(p t) -> p t", t=PACK))
+
         v_codes = [keep.tile([P, S], U32, name=f"v_codes{a}", align_bytes=64) for a in range(PASSES)]
         v_planes = keep.tile([P, S], U8, name="v_planes", align_bytes=64)
         nc.vector.tensor_copy(out=v_codes[0][:], in_=tab_win[0][:].indirect(offsets[:]))
         nc.vector.tensor_copy(out=v_planes[:], in_=tab_planes[:].indirect(offsets[:]))
-        nc.vector.tensor_copy(out=v_codes[1][:], in_=tab_win[1][:].indirect(offsets[:]))
+
+        g_win = [load_g(0), load_g(1)]
         nc.sync.dma_start(
             out=v_plane1[0:SHIFT_ROWS, :].bitcast(I32),
             in_=v_planes[4 : 4 + SHIFT_ROWS, :].bitcast(I32),
         )
-
-        g_win = []
-        g_rows = gT.rearrange("(p t) c -> t p c", t=PACK)
-        for t in range(PACK):
-            win = keep.tile([P, T], F32, name=f"g_win{t}", align_bytes=64)
-            nc.sync.dma_start(out=win[:], in_=g_rows[t])
-            g_win.append(win)
+        g_win.append(load_g(2))
         for q in range(4):
             nc.sync.dma_start(
                 out=w4_planes[32 * q : 32 * q + 4, :, :].bitcast(I32),
@@ -101,12 +108,15 @@ def tile_list_tenant_rank_scales_kernel(
             out=w4_codes[:].bitcast(I32),
             in_=w4_words.rearrange("a p c -> p a c").bitcast(I32),
         )
-        wb_raw = []
+        g_win.append(load_g(3))
+        wb_raw, wb_flat = [], []
         wb_rows = wb.rearrange("(p j) n -> p j n", j=PACK)
-        for c in range(N // WB_COLS):
-            raw = keep.tile([P, PACK, WB_COLS], F32, name=f"wb_raw{c}")
-            nc.sync.dma_start(out=raw[:], in_=wb_rows[:, :, c * WB_COLS : (c + 1) * WB_COLS])
+        for c in range(N // WB_LOAD):
+            flat = keep.tile([P, PACK * HALF], F32, name=f"wb_raw{c}")
+            raw = flat[:].rearrange("p (j n) -> p j n", j=PACK)[:, :, :WB_LOAD]
+            nc.sync.dma_start(out=raw, in_=wb_rows[:, :, c * WB_LOAD : (c + 1) * WB_LOAD])
             wb_raw.append(raw)
+            wb_flat.append(flat)
 
         bo_bank = psum.tile([P, P], F32, name="bo_bank", tag="bank7")
         nc.tensor.transpose(bo_bank[:], bo_rows[:], ident[:])
@@ -116,30 +126,36 @@ def tile_list_tenant_rank_scales_kernel(
         wa_codes, wa_planes = [], []
         for a in range(PASSES):
             woven = keep.tile([P, PACK * R], BF16, name=f"wa_woven{a}", align_bytes=64)
-            nc.scalar.copy(
-                out=woven[:].rearrange("p (t m j) -> p m j t", t=PACK, j=PACK),
-                in_=wa_raw[a][:].rearrange("p j (m t) -> p m j t", t=PACK),
-            )
+            dst = woven[:].rearrange("p (t m j) -> p m j t", t=PACK, j=PACK)
+            src = wa_raw[a][:].rearrange("p j (m t) -> p m j t", t=PACK)
+            if a == 0:
+                nc.scalar.copy(out=dst, in_=src)
+            else:
+                nc.scalar.copy(out=dst[:, : P // 2], in_=src[:, : P // 2])
+                nc.vector.tensor_copy(out=dst[:, P // 2 :], in_=src[:, P // 2 :])
             codes = keep.tile([P, R], U32, name=f"wa_codes{a}", align_bytes=64)
             plane = keep.tile([P, R], U8, name=f"wa_plane{a}", align_bytes=64)
             nc.vector.quantize_mx(out=codes[:].bitcast(FP8X4), scales=plane[:], in_=woven[:])
             wa_codes.append(codes)
             wa_planes.append(plane)
 
-        a4 = [keep.tile([P, PACK * HALF], F32, name=f"a4_{h}")[:] for h in range(HALVES)]
-        g4 = [keep.tile([P, PACK * HALF], F32, name=f"g4_{h}", align_bytes=64)[:] for h in range(HALVES)]
-        h_woven = [keep.tile([P, PACK * HALF], BF16, name=f"h_woven{h}", align_bytes=64)[:] for h in range(HALVES)]
-        wb_woven = [
-            g4[1][:, (PACK - 1) * HALF :].bitcast(BF16),
-            h_woven[1][:, : PACK * WB_COLS],
-            keep.tile([P, PACK * WB_COLS], BF16, name="wb_woven2", align_bytes=64)[:],
-            keep.tile([P, PACK * WB_COLS], BF16, name="wb_woven3", align_bytes=64)[:],
-        ]
+        def half_list(h):
+            return offsets[:, h * (HALF // 16) : (h + 1) * (HALF // 16)]
+
         for h in range(HALVES):
-            cols = slice(h * HALF, (h + 1) * HALF)
+            nc.vector.tensor_copy(
+                out=v_codes[1][:, h * HALF : (h + 1) * HALF], in_=tab_win[1][:].indirect(half_list(h))
+            )
+
+        a_sb = {}
+        a_banks = {}
+        for a in range(PASSES):
             for t in range(PACK):
-                bank = psum.tile([P, HALF], F32, name=f"a_bank{h}_{t}", tag=f"bank{PACK * h + t}")
-                for a in range(PASSES):
+                for h in range(HALVES):
+                    cols = slice(h * HALF, (h + 1) * HALF)
+                    if a == 0:
+                        a_banks[h, t] = psum.tile([P, HALF], F32, name=f"a_bank{h}_{t}", tag=f"bank{HALVES * t + h}")
+                    bank = a_banks[h, t]
                     nc.tensor.matmul_mx(
                         out=bank[:],
                         lhsT=wa_codes[a][:, t * P : (t + 1) * P].bitcast(FP8X4),
@@ -149,78 +165,126 @@ def tile_list_tenant_rank_scales_kernel(
                         start=(a == 0),
                         stop=(a == PASSES - 1),
                     )
-                nc.scalar.activation(
-                    out=a4[h][:, t * HALF : (t + 1) * HALF], in_=bank[:], func=IDENTITY, bias=ba_cols[:, t : t + 1]
-                )
+                    if a == PASSES - 1:
+                        a_sb[h, t] = keep.tile([P, HALF], F32, name=f"a_sb{h}_{t}")
+                        nc.scalar.activation(
+                            out=a_sb[h, t][:], in_=bank[:], func=IDENTITY, bias=ba_cols[:, t : t + 1]
+                        )
 
+        h4 = [keep.tile([P, PACK * HALF], F32, name=f"h4_{h}", align_bytes=64)[:] for h in range(HALVES)]
+        h_woven = [
+            keep.tile([P, PACK * HALF], BF16, name="h_woven0", align_bytes=64)[:],
+            keep.tile([P, PACK * HALF], BF16, name="h_woven1", align_bytes=64)[:],
+        ]
+        wb_woven = [
+            keep.tile([P, PACK * WB_COLS], BF16, name="wb_woven0", align_bytes=64)[:],
+            keep.tile([P, PACK * WB_COLS], BF16, name="wb_woven1", align_bytes=64)[:],
+            h4[1][:, 3 * HALF :].bitcast(BF16),
+            h_woven[1][:, : PACK * WB_COLS],
+        ]
 
-        def gather_g(h, t):
-            lists = offsets[:, h * (HALF // 16) : (h + 1) * (HALF // 16)]
-            nc.vector.tensor_copy(out=g4[h][:, t * HALF : (t + 1) * HALF], in_=g_win[t][:].indirect(lists))
+        shared_planes = keep.tile([P, HALF], U8, name="shared_planes", align_bytes=64)
+
+        def scale_ranks(h, t):
+            nc.vector.tensor_tensor(
+                out=h4[h][:, t * HALF : (t + 1) * HALF],
+                in0=g_win[t][:].indirect(half_list(h)),
+                in1=a_sb[h, t][:],
+                op=MULT,
+            )
 
         def make_h(h):
             woven = h_woven[h]
-            nc.vector.tensor_tensor(
-                out=woven[:].rearrange("p (c i t) -> p c t i", i=4, t=PACK),
-                in0=a4[h].rearrange("p (t c i) -> p c t i", t=PACK, i=4),
-                in1=g4[h].rearrange("p (t c i) -> p c t i", t=PACK, i=4),
-                op=MULT,
+            nc.vector.tensor_copy(
+                out=woven.rearrange("p (c i t) -> p c t i", i=4, t=PACK),
+                in_=h4[h].rearrange("p (t c i) -> p c t i", t=PACK, i=4),
             )
-            codes = keep.tile([P, HALF], U32, name=f"h_codes{h}", align_bytes=64)
-            plane = keep.tile([P, HALF], U8, name=f"h_plane{h}", align_bytes=64)
-            nc.vector.quantize_mx(out=codes[:].bitcast(FP8X4), scales=plane[:], in_=woven[:])
+
+        def quantise_h(h):
+            woven = h_woven[h]
+            if h == 0:
+                codes = keep.tile([P, HALF], U32, name="h_codes0", align_bytes=64)[:]
+                plane = shared_planes[4:P, :]
+            else:
+                codes = keep.tile([P, HALF], U32, name="h_codes1", align_bytes=64)[:]
+                plane = w4_codes[:, 1, HALF : 2 * HALF]
+            nc.vector.quantize_mx(out=codes.bitcast(FP8X4), scales=plane, in_=woven)
             return codes, plane
 
         def quantise_wb(c):
             woven = wb_woven[c]
-            nc.scalar.copy(
-                out=woven[:].rearrange("p (c i j) -> p c j i", i=4, j=PACK),
-                in_=wb_raw[c][:].rearrange("p j (c i) -> p c j i", i=4),
+            load, c0 = divmod(c * WB_COLS, WB_LOAD)
+            weave = nc.vector.tensor_copy if c == N // WB_COLS - 1 else nc.scalar.copy
+            weave(
+                out=woven.rearrange("p (c i j) -> p c j i", i=4, j=PACK),
+                in_=wb_raw[load][:, :, c0 : c0 + WB_COLS].rearrange("p j (c i) -> p c j i", i=4),
             )
             codes = keep.tile([P, WB_COLS], U32, name=f"wb_codes{c}", align_bytes=64)
-            plane = keep.tile([P, WB_COLS], U8, name=f"wb_plane{c}", align_bytes=64)
-            nc.vector.quantize_mx(out=codes[:].bitcast(FP8X4), scales=plane[:], in_=woven[:])
+            if c == 0:
+                plane = shared_planes[:, :WB_COLS]
+            else:
+                plane = keep.tile([P, WB_COLS], U8, name=f"wb_plane{c}", align_bytes=64)[:]
+            nc.vector.quantize_mx(out=codes[:].bitcast(FP8X4), scales=plane, in_=woven)
             return codes, plane
 
         for t in range(PACK - 1):
             for h in range(HALVES):
-                gather_g(h, t)
-        gather_g(0, PACK - 1)
-        h_mx = [make_h(0)]
-        wb_mx = [quantise_wb(c) for c in range(N // WB_COLS)]
-        gather_g(1, PACK - 1)
-        h_mx.append(make_h(1))
+                scale_ranks(h, t)
+        scale_ranks(0, 3)
+        make_h(0)
+        wb_mx = [quantise_wb(0)]
+        h_mx = [quantise_h(0)]
+        wb_mx.extend(quantise_wb(c) for c in range(1, N // WB_COLS))
 
         v_scales = [v_planes, v_plane1]
-        for h in range(HALVES):
+        banks = {}
+
+        def base_passes(h, n):
             cols = slice(h * HALF, (h + 1) * HALF)
-            for n in range(N_TILES):
-                bank = psum.tile([P, HALF], F32, name=f"y_bank{h}_{n}", tag=f"bank{n}")
-                for a in range(PASSES):
-                    nc.tensor.matmul_mx(
-                        out=bank[:],
-                        lhsT=w4_codes[:, a, 2 * n * P : 2 * (n + 1) * P].bitcast(FP4X4),
-                        lhsT_scale=w4_planes[:, a, n * P : (n + 1) * P],
-                        rhs=v_codes[a][:, cols].bitcast(FP8X4),
-                        rhs_scale=v_scales[a][:, cols],
-                        start=(a == 0),
-                        stop=False,
-                    )
-                c, m0 = divmod(n * P, WB_COLS)
+            banks[h, n] = psum.tile([P, HALF], F32, name=f"y_bank{h}_{n}", tag=f"bank{n}")
+            for a in range(PASSES):
                 nc.tensor.matmul_mx(
-                    out=bank[:],
-                    lhsT=wb_mx[c][0][:, m0 : m0 + P].bitcast(FP8X4),
-                    lhsT_scale=wb_mx[c][1][:, m0 : m0 + P],
-                    rhs=h_mx[h][0][:].bitcast(FP8X4),
-                    rhs_scale=h_mx[h][1][:],
-                    start=False,
-                    stop=True,
+                    out=banks[h, n][:],
+                    lhsT=w4_codes[:, a, 2 * n * P : 2 * (n + 1) * P].bitcast(FP4X4),
+                    lhsT_scale=w4_planes[:, a, n * P : (n + 1) * P],
+                    rhs=v_codes[a][:, cols].bitcast(FP8X4),
+                    rhs_scale=v_scales[a][:, cols],
+                    start=(a == 0),
+                    stop=False,
                 )
-                result = keep.tile([P, HALF], F32, name=f"result{h}_{n}")
-                if h == 1 and n % 2 == 0:
-                    nc.vector.tensor_scalar_add(out=result[:], in0=bank[:], scalar1=bo_cols[:, n : n + 1])
-                else:
-                    nc.scalar.activation(
-                        out=result[:], in_=bank[:], func=IDENTITY, bias=bo_cols[:, n : n + 1]
-                    )
-                nc.sync.dma_start(out=out[n * P : (n + 1) * P, cols], in_=result[:])
+
+        def close(h, n):
+            bank = banks[h, n]
+            c, m0 = divmod(n * P, WB_COLS)
+            nc.tensor.matmul_mx(
+                out=bank[:],
+                lhsT=wb_mx[c][0][:, m0 : m0 + P].bitcast(FP8X4),
+                lhsT_scale=wb_mx[c][1][:, m0 : m0 + P],
+                rhs=h_mx[h][0].bitcast(FP8X4),
+                rhs_scale=h_mx[h][1],
+                start=False,
+                stop=True,
+            )
+            if h == 0 and n < PACK:
+                result = wb_flat[2][:, n * HALF : (n + 1) * HALF]
+            else:
+                result = keep.tile([P, HALF], F32, name=f"result{h}_{n}")[:]
+            if (h == 1 and n % 2 == 0) or (h == 0 and n == N_TILES - 1):
+                nc.vector.tensor_scalar_add(out=result, in0=bank[:], scalar1=bo_cols[:, n : n + 1])
+            else:
+                nc.scalar.activation(out=result, in_=bank[:], func=IDENTITY, bias=bo_cols[:, n : n + 1])
+            nc.sync.dma_start(out=out[n * P : (n + 1) * P, h * HALF : (h + 1) * HALF], in_=result)
+
+        for n in range(N_TILES):
+            base_passes(0, n)
+        for n in range(N_TILES):
+            close(0, n)
+        for n in range(AHEAD):
+            base_passes(1, n)
+        scale_ranks(1, PACK - 1)
+        make_h(1)
+        h_mx.append(quantise_h(1))
+        for n in range(N_TILES):
+            if n >= AHEAD:
+                base_passes(1, n)
+            close(1, n)

@@ -24,8 +24,7 @@ PASSES = K // K_PASS
 HALF = 512
 HALVES = S // HALF
 N_TILES = N // P
-WB_LOAD = 256
-WB_COLS = 256
+WB_PIECES = ((0, 256), (256, 256), (512, 256), (768, 256))
 SHIFT_ROWS = 112
 AHEAD = 4
 
@@ -93,30 +92,36 @@ def tile_list_tenant_rank_scales_kernel(
         nc.vector.tensor_copy(out=v_planes[:], in_=tab_planes[:].indirect(offsets[:]))
 
         g_win = [load_g(0), load_g(1)]
+        g_win.append(load_g(2))
+        for r in range(4):
+            nc.sync.dma_start(
+                out=w4_planes[r:P:32, :, :].bitcast(I32),
+                in_=w4_scales[:, r:16:4, :].rearrange("a q c -> q a c").bitcast(I32),
+            )
+
+        def load_w4(a):
+            codes = keep.tile([P, 2 * N], U8, name=f"w4_codes{a}", align_bytes=64)
+            nc.sync.dma_start(out=codes[:].bitcast(I32), in_=w4_words[a].bitcast(I32))
+            return codes
+
+        w4_codes = [load_w4(0)]
+        g_win.append(load_g(3))
+        wb_rows = wb.rearrange("(p j) n -> p j n", j=PACK)
+
+        def load_wb(c):
+            c0, width = WB_PIECES[c]
+            flat = keep.tile([P, PACK * HALF], F32, name=f"wb_raw{c}")
+            raw = flat[:].rearrange("p (j n) -> p j n", j=PACK)[:, :, :width]
+            nc.sync.dma_start(out=raw, in_=wb_rows[:, :, c0 : c0 + width])
+            return flat, raw
+
+        wb_raw = [load_wb(0)]
         nc.sync.dma_start(
             out=v_plane1[0:SHIFT_ROWS, :].bitcast(I32),
             in_=v_planes[4 : 4 + SHIFT_ROWS, :].bitcast(I32),
         )
-        g_win.append(load_g(2))
-        for q in range(4):
-            nc.sync.dma_start(
-                out=w4_planes[32 * q : 32 * q + 4, :, :].bitcast(I32),
-                in_=w4_scales[:, 4 * q : 4 * q + 4, :].rearrange("a r c -> r a c").bitcast(I32),
-            )
-        w4_codes = keep.tile([P, PASSES, 2 * N], U8, name="w4_codes", align_bytes=64)
-        nc.sync.dma_start(
-            out=w4_codes[:].bitcast(I32),
-            in_=w4_words.rearrange("a p c -> p a c").bitcast(I32),
-        )
-        g_win.append(load_g(3))
-        wb_raw, wb_flat = [], []
-        wb_rows = wb.rearrange("(p j) n -> p j n", j=PACK)
-        for c in range(N // WB_LOAD):
-            flat = keep.tile([P, PACK * HALF], F32, name=f"wb_raw{c}")
-            raw = flat[:].rearrange("p (j n) -> p j n", j=PACK)[:, :, :WB_LOAD]
-            nc.sync.dma_start(out=raw, in_=wb_rows[:, :, c * WB_LOAD : (c + 1) * WB_LOAD])
-            wb_raw.append(raw)
-            wb_flat.append(flat)
+        w4_codes.append(load_w4(1))
+        wb_raw.extend([load_wb(1), load_wb(2), load_wb(3)])
 
         bo_bank = psum.tile([P, P], F32, name="bo_bank", tag="bank7")
         nc.tensor.transpose(bo_bank[:], bo_rows[:], ident[:])
@@ -177,10 +182,10 @@ def tile_list_tenant_rank_scales_kernel(
             keep.tile([P, PACK * HALF], BF16, name="h_woven1", align_bytes=64)[:],
         ]
         wb_woven = [
-            keep.tile([P, PACK * WB_COLS], BF16, name="wb_woven0", align_bytes=64)[:],
-            keep.tile([P, PACK * WB_COLS], BF16, name="wb_woven1", align_bytes=64)[:],
-            h4[1][:, 3 * HALF :].bitcast(BF16),
-            h_woven[1][:, : PACK * WB_COLS],
+            keep.tile([P, PACK * WB_PIECES[0][1]], BF16, name="wb_woven0", align_bytes=64)[:],
+            keep.tile([P, PACK * WB_PIECES[1][1]], BF16, name="wb_woven1", align_bytes=64)[:],
+            h4[1][:, (PACK - 1) * HALF :].bitcast(BF16),
+            h_woven[1][:, : PACK * WB_PIECES[3][1]],
         ]
 
         shared_planes = keep.tile([P, HALF], U8, name="shared_planes", align_bytes=64)
@@ -207,23 +212,23 @@ def tile_list_tenant_rank_scales_kernel(
                 plane = shared_planes[4:P, :]
             else:
                 codes = keep.tile([P, HALF], U32, name="h_codes1", align_bytes=64)[:]
-                plane = w4_codes[:, 1, HALF : 2 * HALF]
+                plane = w4_codes[1][:, HALF : 2 * HALF]
             nc.vector.quantize_mx(out=codes.bitcast(FP8X4), scales=plane, in_=woven)
             return codes, plane
 
         def quantise_wb(c):
+            width = WB_PIECES[c][1]
             woven = wb_woven[c]
-            load, c0 = divmod(c * WB_COLS, WB_LOAD)
-            weave = nc.vector.tensor_copy if c == N // WB_COLS - 1 else nc.scalar.copy
+            weave = nc.vector.tensor_copy if c == 3 else nc.scalar.copy
             weave(
                 out=woven.rearrange("p (c i j) -> p c j i", i=4, j=PACK),
-                in_=wb_raw[load][:, :, c0 : c0 + WB_COLS].rearrange("p j (c i) -> p c j i", i=4),
+                in_=wb_raw[c][1].rearrange("p j (c i) -> p c j i", i=4),
             )
-            codes = keep.tile([P, WB_COLS], U32, name=f"wb_codes{c}", align_bytes=64)
+            codes = keep.tile([P, width], U32, name=f"wb_codes{c}", align_bytes=64)
             if c == 0:
-                plane = shared_planes[:, :WB_COLS]
+                plane = shared_planes[:, :width]
             else:
-                plane = keep.tile([P, WB_COLS], U8, name=f"wb_plane{c}", align_bytes=64)[:]
+                plane = keep.tile([P, width], U8, name=f"wb_plane{c}", align_bytes=64)[:]
             nc.vector.quantize_mx(out=codes[:].bitcast(FP8X4), scales=plane, in_=woven)
             return codes, plane
 
@@ -234,7 +239,7 @@ def tile_list_tenant_rank_scales_kernel(
         make_h(0)
         wb_mx = [quantise_wb(0)]
         h_mx = [quantise_h(0)]
-        wb_mx.extend(quantise_wb(c) for c in range(1, N // WB_COLS))
+        wb_mx.extend([quantise_wb(1), quantise_wb(2), quantise_wb(3)])
 
         v_scales = [v_planes, v_plane1]
         banks = {}
@@ -245,7 +250,7 @@ def tile_list_tenant_rank_scales_kernel(
             for a in range(PASSES):
                 nc.tensor.matmul_mx(
                     out=banks[h, n][:],
-                    lhsT=w4_codes[:, a, 2 * n * P : 2 * (n + 1) * P].bitcast(FP4X4),
+                    lhsT=w4_codes[a][:, 2 * n * P : 2 * (n + 1) * P].bitcast(FP4X4),
                     lhsT_scale=w4_planes[:, a, n * P : (n + 1) * P],
                     rhs=v_codes[a][:, cols].bitcast(FP8X4),
                     rhs_scale=v_scales[a][:, cols],
@@ -255,7 +260,8 @@ def tile_list_tenant_rank_scales_kernel(
 
         def close(h, n):
             bank = banks[h, n]
-            c, m0 = divmod(n * P, WB_COLS)
+            c = max(k for k in range(len(WB_PIECES)) if WB_PIECES[k][0] <= n * P)
+            m0 = n * P - WB_PIECES[c][0]
             nc.tensor.matmul_mx(
                 out=bank[:],
                 lhsT=wb_mx[c][0][:, m0 : m0 + P].bitcast(FP8X4),
@@ -266,7 +272,7 @@ def tile_list_tenant_rank_scales_kernel(
                 stop=True,
             )
             if h == 0 and n < PACK:
-                result = wb_flat[2][:, n * HALF : (n + 1) * HALF]
+                result = wb_raw[2][0][:, n * HALF : (n + 1) * HALF]
             else:
                 result = keep.tile([P, HALF], F32, name=f"result{h}_{n}")[:]
             if (h == 1 and n % 2 == 0) or (h == 0 and n == N_TILES - 1):

@@ -21,12 +21,17 @@ P = 128
 PACK = 4
 K_PASS = P * PACK
 PASSES = K // K_PASS
+QUADRANT = 32
+SCALE_ROWS = K_PASS // 32
+LIST_ROWS = 16
+LINE = 4
 HALF = 512
 HALVES = S // HALF
 N_TILES = N // P
-WB_PIECES = ((0, 256), (256, 256), (512, 256), (768, 256))
+WB_COLS = 256
+WB_PIECES = N // WB_COLS
 SHIFT_ROWS = 112
-AHEAD = 4
+AHEAD = 3
 
 
 def tile_list_tenant_rank_scales_kernel(
@@ -37,7 +42,7 @@ def tile_list_tenant_rank_scales_kernel(
         keep = ctx.enter_context(tc.tile_pool(name="keep", bufs=1))
         psum = ctx.enter_context(tc.psum_pool(name="psum", bufs=1))
 
-        offsets = keep.tile([P, S // 16], U16, name="offsets")
+        offsets = keep.tile([P, S // LIST_ROWS], U16, name="offsets")
         nc.sync.dma_start(offsets[:], offs)
 
         tab_planes = keep.tile([P, T], U8, name="tab_planes", align_bytes=64)
@@ -75,10 +80,23 @@ def tile_list_tenant_rank_scales_kernel(
             nc.sync.dma_start(out=win[:], in_=g_rows[t])
             return win
 
+        def load_w4(a):
+            codes = keep.tile([P, 2 * N], U8, name=f"w4_codes{a}", align_bytes=64)
+            nc.sync.dma_start(out=codes[:].bitcast(I32), in_=w4_words[a].bitcast(I32))
+            return codes
+
+        wb_rows = wb.rearrange("(p j) n -> p j n", j=PACK)
+
+        def load_wb(c):
+            flat = keep.tile([P, PACK * HALF], F32, name=f"wb_raw{c}")
+            raw = flat[:].rearrange("p (j n) -> p j n", j=PACK)[:, :, :WB_COLS]
+            nc.sync.dma_start(out=raw, in_=wb_rows[:, :, c * WB_COLS : (c + 1) * WB_COLS])
+            return flat, raw
+
         tab_win = [load_table(0)]
-        for q in range(4):
+        for q in range(P // QUADRANT):
             nc.sync.dma_start(
-                out=tab_planes[32 * q : 32 * q + 8, :].bitcast(I32),
+                out=tab_planes[QUADRANT * q : QUADRANT * q + PASSES * 4, :].bitcast(I32),
                 in_=tab_scales[:, 4 * q : 4 * q + 4, :].bitcast(I32),
             )
         nc.sync.dma_start(out=bo_rows[0:N_TILES, :], in_=bo.rearrange("(c p) -> c p", p=P))
@@ -91,39 +109,23 @@ def tile_list_tenant_rank_scales_kernel(
         nc.vector.tensor_copy(out=v_codes[0][:], in_=tab_win[0][:].indirect(offsets[:]))
         nc.vector.tensor_copy(out=v_planes[:], in_=tab_planes[:].indirect(offsets[:]))
 
-        g_win = [load_g(0), load_g(1)]
-        g_win.append(load_g(2))
+        g_win = [load_g(t) for t in range(PACK - 1)]
         for r in range(4):
             nc.sync.dma_start(
-                out=w4_planes[r:P:32, :, :].bitcast(I32),
-                in_=w4_scales[:, r:16:4, :].rearrange("a q c -> q a c").bitcast(I32),
+                out=w4_planes[r:P:QUADRANT, :, :].bitcast(I32),
+                in_=w4_scales[:, r:SCALE_ROWS:4, :].rearrange("a q c -> q a c").bitcast(I32),
             )
-
-        def load_w4(a):
-            codes = keep.tile([P, 2 * N], U8, name=f"w4_codes{a}", align_bytes=64)
-            nc.sync.dma_start(out=codes[:].bitcast(I32), in_=w4_words[a].bitcast(I32))
-            return codes
-
         w4_codes = [load_w4(0)]
-        g_win.append(load_g(3))
-        wb_rows = wb.rearrange("(p j) n -> p j n", j=PACK)
-
-        def load_wb(c):
-            c0, width = WB_PIECES[c]
-            flat = keep.tile([P, PACK * HALF], F32, name=f"wb_raw{c}")
-            raw = flat[:].rearrange("p (j n) -> p j n", j=PACK)[:, :, :width]
-            nc.sync.dma_start(out=raw, in_=wb_rows[:, :, c0 : c0 + width])
-            return flat, raw
-
+        g_win.append(load_g(PACK - 1))
         wb_raw = [load_wb(0)]
         nc.sync.dma_start(
             out=v_plane1[0:SHIFT_ROWS, :].bitcast(I32),
             in_=v_planes[4 : 4 + SHIFT_ROWS, :].bitcast(I32),
         )
         w4_codes.append(load_w4(1))
-        wb_raw.extend([load_wb(1), load_wb(2), load_wb(3)])
+        wb_raw.extend([load_wb(c) for c in range(1, WB_PIECES)])
 
-        bo_bank = psum.tile([P, P], F32, name="bo_bank", tag="bank7")
+        bo_bank = psum.tile([P, P], F32, name="bo_bank", tag=f"bank{N_TILES - 1}")
         nc.tensor.transpose(bo_bank[:], bo_rows[:], ident[:])
         bo_cols = keep.tile([P, N_TILES], F32, name="bo_cols")
         nc.scalar.activation(out=bo_cols[:], in_=bo_bank[:, 0:N_TILES], func=IDENTITY)
@@ -145,7 +147,7 @@ def tile_list_tenant_rank_scales_kernel(
             wa_planes.append(plane)
 
         def half_list(h):
-            return offsets[:, h * (HALF // 16) : (h + 1) * (HALF // 16)]
+            return offsets[:, h * (HALF // LIST_ROWS) : (h + 1) * (HALF // LIST_ROWS)]
 
         for h in range(HALVES):
             nc.vector.tensor_copy(
@@ -177,17 +179,13 @@ def tile_list_tenant_rank_scales_kernel(
                         )
 
         h4 = [keep.tile([P, PACK * HALF], F32, name=f"h4_{h}", align_bytes=64)[:] for h in range(HALVES)]
-        h_woven = [
-            keep.tile([P, PACK * HALF], BF16, name="h_woven0", align_bytes=64)[:],
-            keep.tile([P, PACK * HALF], BF16, name="h_woven1", align_bytes=64)[:],
-        ]
+        h_woven = [keep.tile([P, PACK * HALF], BF16, name=f"h_woven{h}", align_bytes=64)[:] for h in range(HALVES)]
         wb_woven = [
-            keep.tile([P, PACK * WB_PIECES[0][1]], BF16, name="wb_woven0", align_bytes=64)[:],
-            keep.tile([P, PACK * WB_PIECES[1][1]], BF16, name="wb_woven1", align_bytes=64)[:],
+            keep.tile([P, PACK * WB_COLS], BF16, name="wb_woven0", align_bytes=64)[:],
+            keep.tile([P, PACK * WB_COLS], BF16, name="wb_woven1", align_bytes=64)[:],
             h4[1][:, (PACK - 1) * HALF :].bitcast(BF16),
-            h_woven[1][:, : PACK * WB_PIECES[3][1]],
+            h_woven[1][:, : PACK * WB_COLS],
         ]
-
         shared_planes = keep.tile([P, HALF], U8, name="shared_planes", align_bytes=64)
 
         def scale_ranks(h, t):
@@ -198,58 +196,53 @@ def tile_list_tenant_rank_scales_kernel(
                 op=MULT,
             )
 
-        def make_h(h):
-            woven = h_woven[h]
+        def weave_h(h):
             nc.vector.tensor_copy(
-                out=woven.rearrange("p (c i t) -> p c t i", i=4, t=PACK),
-                in_=h4[h].rearrange("p (t c i) -> p c t i", t=PACK, i=4),
+                out=h_woven[h].rearrange("p (c i t) -> p c t i", i=LINE, t=PACK),
+                in_=h4[h].rearrange("p (t c i) -> p c t i", t=PACK, i=LINE),
             )
 
         def quantise_h(h):
-            woven = h_woven[h]
+            codes = keep.tile([P, HALF], U32, name=f"h_codes{h}", align_bytes=64)[:]
             if h == 0:
-                codes = keep.tile([P, HALF], U32, name="h_codes0", align_bytes=64)[:]
                 plane = shared_planes[4:P, :]
             else:
-                codes = keep.tile([P, HALF], U32, name="h_codes1", align_bytes=64)[:]
-                plane = w4_codes[1][:, HALF : 2 * HALF]
-            nc.vector.quantize_mx(out=codes.bitcast(FP8X4), scales=plane, in_=woven)
+                plane = w4_codes[1][:, (AHEAD - 2) * 2 * P : AHEAD * 2 * P]
+            nc.vector.quantize_mx(out=codes.bitcast(FP8X4), scales=plane, in_=h_woven[h])
             return codes, plane
 
         def quantise_wb(c):
-            width = WB_PIECES[c][1]
-            woven = wb_woven[c]
-            weave = nc.vector.tensor_copy if c == 3 else nc.scalar.copy
+            weave = nc.vector.tensor_copy if c == WB_PIECES - 1 else nc.scalar.copy
             weave(
-                out=woven.rearrange("p (c i j) -> p c j i", i=4, j=PACK),
-                in_=wb_raw[c][1].rearrange("p j (c i) -> p c j i", i=4),
+                out=wb_woven[c].rearrange("p (c i j) -> p c j i", i=LINE, j=PACK),
+                in_=wb_raw[c][1].rearrange("p j (c i) -> p c j i", i=LINE),
             )
-            codes = keep.tile([P, width], U32, name=f"wb_codes{c}", align_bytes=64)
+            codes = keep.tile([P, WB_COLS], U32, name=f"wb_codes{c}", align_bytes=64)
             if c == 0:
-                plane = shared_planes[:, :width]
+                plane = shared_planes[:, :WB_COLS]
             else:
-                plane = keep.tile([P, width], U8, name=f"wb_plane{c}", align_bytes=64)[:]
-            nc.vector.quantize_mx(out=codes[:].bitcast(FP8X4), scales=plane, in_=woven)
+                plane = keep.tile([P, WB_COLS], U8, name=f"wb_plane{c}", align_bytes=64)[:]
+            nc.vector.quantize_mx(out=codes[:].bitcast(FP8X4), scales=plane, in_=wb_woven[c])
             return codes, plane
 
         for t in range(PACK - 1):
             for h in range(HALVES):
                 scale_ranks(h, t)
-        scale_ranks(0, 3)
-        make_h(0)
+        scale_ranks(0, PACK - 1)
+        weave_h(0)
         wb_mx = [quantise_wb(0)]
         h_mx = [quantise_h(0)]
-        wb_mx.extend([quantise_wb(1), quantise_wb(2), quantise_wb(3)])
+        wb_mx.extend([quantise_wb(c) for c in range(1, WB_PIECES)])
 
         v_scales = [v_planes, v_plane1]
-        banks = {}
+        y_banks = {}
 
         def base_passes(h, n):
             cols = slice(h * HALF, (h + 1) * HALF)
-            banks[h, n] = psum.tile([P, HALF], F32, name=f"y_bank{h}_{n}", tag=f"bank{n}")
+            y_banks[h, n] = psum.tile([P, HALF], F32, name=f"y_bank{h}_{n}", tag=f"bank{n}")
             for a in range(PASSES):
                 nc.tensor.matmul_mx(
-                    out=banks[h, n][:],
+                    out=y_banks[h, n][:],
                     lhsT=w4_codes[a][:, 2 * n * P : 2 * (n + 1) * P].bitcast(FP4X4),
                     lhsT_scale=w4_planes[:, a, n * P : (n + 1) * P],
                     rhs=v_codes[a][:, cols].bitcast(FP8X4),
@@ -259,9 +252,8 @@ def tile_list_tenant_rank_scales_kernel(
                 )
 
         def close(h, n):
-            bank = banks[h, n]
-            c = max(k for k in range(len(WB_PIECES)) if WB_PIECES[k][0] <= n * P)
-            m0 = n * P - WB_PIECES[c][0]
+            bank = y_banks[h, n]
+            c, m0 = divmod(n * P, WB_COLS)
             nc.tensor.matmul_mx(
                 out=bank[:],
                 lhsT=wb_mx[c][0][:, m0 : m0 + P].bitcast(FP8X4),
@@ -272,7 +264,7 @@ def tile_list_tenant_rank_scales_kernel(
                 stop=True,
             )
             if h == 0 and n < PACK:
-                result = wb_raw[2][0][:, n * HALF : (n + 1) * HALF]
+                result = wb_raw[WB_PIECES - 2][0][:, n * HALF : (n + 1) * HALF]
             else:
                 result = keep.tile([P, HALF], F32, name=f"result{h}_{n}")[:]
             if (h == 1 and n % 2 == 0) or (h == 0 and n == N_TILES - 1):
@@ -288,7 +280,7 @@ def tile_list_tenant_rank_scales_kernel(
         for n in range(AHEAD):
             base_passes(1, n)
         scale_ranks(1, PACK - 1)
-        make_h(1)
+        weave_h(1)
         h_mx.append(quantise_h(1))
         for n in range(N_TILES):
             if n >= AHEAD:

@@ -28,10 +28,16 @@ LINE = 4
 HALF = 512
 HALVES = S // HALF
 N_TILES = N // P
+QUARTER = HALF // 2
 WB_COLS = 256
-WB_PIECES = N // WB_COLS
+EARLY = N_TILES // 2
+EARLY_COLS = EARLY * P
+W4_FIRST = EARLY + 1
 SHIFT_ROWS = 112
-AHEAD = 3
+
+
+WA_SCALAR = (96, 56)
+REUSE = {(h, n): HALVES * ((2 * (n - EARLY) + h) % EARLY) + (2 * (n - EARLY) + h) // EARLY for n in range(EARLY, N_TILES) for h in range(HALVES)}
 
 
 def tile_list_tenant_rank_scales_kernel(
@@ -40,6 +46,7 @@ def tile_list_tenant_rank_scales_kernel(
     nc = tc.nc
     with ExitStack() as ctx:
         keep = ctx.enter_context(tc.tile_pool(name="keep", bufs=1))
+        shared = ctx.enter_context(tc.tile_pool(name="shared", bufs=1))
         psum = ctx.enter_context(tc.psum_pool(name="psum", bufs=1))
 
         offsets = keep.tile([P, S // LIST_ROWS], U16, name="offsets")
@@ -80,17 +87,17 @@ def tile_list_tenant_rank_scales_kernel(
             nc.sync.dma_start(out=win[:], in_=g_rows[t])
             return win
 
-        def load_w4(a):
-            codes = keep.tile([P, 2 * N], U8, name=f"w4_codes{a}", align_bytes=64)
-            nc.sync.dma_start(out=codes[:].bitcast(I32), in_=w4_words[a].bitcast(I32))
+        def load_w4_early(a):
+            codes = keep.tile([P, 2 * W4_FIRST * P], U8, name=f"w4_early{a}", align_bytes=64)
+            nc.sync.dma_start(out=codes[:].bitcast(I32), in_=w4_words[a][:, : 2 * W4_FIRST * P].bitcast(I32))
             return codes
 
         wb_rows = wb.rearrange("(p j) n -> p j n", j=PACK)
 
-        def load_wb(c):
-            flat = keep.tile([P, PACK * HALF], F32, name=f"wb_raw{c}")
-            raw = flat[:].rearrange("p (j n) -> p j n", j=PACK)[:, :, :WB_COLS]
-            nc.sync.dma_start(out=raw, in_=wb_rows[:, :, c * WB_COLS : (c + 1) * WB_COLS])
+        def load_wb(name, c0, width):
+            flat = keep.tile([P, PACK * HALF], F32, name=name)
+            raw = flat[:].rearrange("p (j n) -> p j n", j=PACK)[:, :, :width]
+            nc.sync.dma_start(out=raw, in_=wb_rows[:, :, c0 : c0 + width])
             return flat, raw
 
         tab_win = [load_table(0)]
@@ -109,21 +116,22 @@ def tile_list_tenant_rank_scales_kernel(
         nc.vector.tensor_copy(out=v_codes[0][:], in_=tab_win[0][:].indirect(offsets[:]))
         nc.vector.tensor_copy(out=v_planes[:], in_=tab_planes[:].indirect(offsets[:]))
 
-        g_win = [load_g(t) for t in range(PACK - 1)]
+        g_win = [load_g(t) for t in range(2)]
+        nc.sync.dma_start(
+            out=v_plane1[0:SHIFT_ROWS, :].bitcast(I32),
+            in_=v_planes[4 : 4 + SHIFT_ROWS, :].bitcast(I32),
+        )
         for r in range(4):
             nc.sync.dma_start(
                 out=w4_planes[r:P:QUADRANT, :, :].bitcast(I32),
                 in_=w4_scales[:, r:SCALE_ROWS:4, :].rearrange("a q c -> q a c").bitcast(I32),
             )
-        w4_codes = [load_w4(0)]
-        g_win.append(load_g(PACK - 1))
-        wb_raw = [load_wb(0)]
-        nc.sync.dma_start(
-            out=v_plane1[0:SHIFT_ROWS, :].bitcast(I32),
-            in_=v_planes[4 : 4 + SHIFT_ROWS, :].bitcast(I32),
-        )
-        w4_codes.append(load_w4(1))
-        wb_raw.extend([load_wb(c) for c in range(1, WB_PIECES)])
+        w4_early = [load_w4_early(0)]
+        g_win.extend([load_g(t) for t in range(2, PACK)])
+        w4_early.append(load_w4_early(1))
+        wb_loads = [load_wb(f"wb_raw{c}", c * WB_COLS, WB_COLS) for c in range(2)]
+        wb_late = load_wb("wb_late", EARLY_COLS, N - EARLY_COLS)[1]
+        wb_raw = [wb_loads[0][1], wb_loads[1][1], wb_late[:, :, :WB_COLS], wb_late[:, :, WB_COLS:]]
 
         bo_bank = psum.tile([P, P], F32, name="bo_bank", tag=f"bank{N_TILES - 1}")
         nc.tensor.transpose(bo_bank[:], bo_rows[:], ident[:])
@@ -135,23 +143,21 @@ def tile_list_tenant_rank_scales_kernel(
             woven = keep.tile([P, PACK * R], BF16, name=f"wa_woven{a}", align_bytes=64)
             dst = woven[:].rearrange("p (t m j) -> p m j t", t=PACK, j=PACK)
             src = wa_raw[a][:].rearrange("p j (m t) -> p m j t", t=PACK)
-            if a == 0:
-                nc.scalar.copy(out=dst, in_=src)
-            else:
-                nc.scalar.copy(out=dst[:, : P // 2], in_=src[:, : P // 2])
-                nc.vector.tensor_copy(out=dst[:, P // 2 :], in_=src[:, P // 2 :])
+            cut = WA_SCALAR[a]
+            nc.scalar.copy(out=dst[:, :cut], in_=src[:, :cut])
+            nc.vector.tensor_copy(out=dst[:, cut:], in_=src[:, cut:])
             codes = keep.tile([P, R], U32, name=f"wa_codes{a}", align_bytes=64)
             plane = keep.tile([P, R], U8, name=f"wa_plane{a}", align_bytes=64)
             nc.vector.quantize_mx(out=codes[:].bitcast(FP8X4), scales=plane[:], in_=woven[:])
             wa_codes.append(codes)
             wa_planes.append(plane)
 
-        def half_list(h):
-            return offsets[:, h * (HALF // LIST_ROWS) : (h + 1) * (HALF // LIST_ROWS)]
+        def part_list(c0, width):
+            return offsets[:, c0 // LIST_ROWS : (c0 + width) // LIST_ROWS]
 
         for h in range(HALVES):
             nc.vector.tensor_copy(
-                out=v_codes[1][:, h * HALF : (h + 1) * HALF], in_=tab_win[1][:].indirect(half_list(h))
+                out=v_codes[1][:, h * HALF : (h + 1) * HALF], in_=tab_win[1][:].indirect(part_list(h * HALF, HALF))
             )
 
         a_sb = {}
@@ -178,84 +184,76 @@ def tile_list_tenant_rank_scales_kernel(
                             out=a_sb[h, t][:], in_=bank[:], func=IDENTITY, bias=ba_cols[:, t : t + 1]
                         )
 
-        h4 = [keep.tile([P, PACK * HALF], F32, name=f"h4_{h}", align_bytes=64)[:] for h in range(HALVES)]
-        h_woven = [keep.tile([P, PACK * HALF], BF16, name=f"h_woven{h}", align_bytes=64)[:] for h in range(HALVES)]
-        wb_woven = [
-            keep.tile([P, PACK * WB_COLS], BF16, name="wb_woven0", align_bytes=64)[:],
-            keep.tile([P, PACK * WB_COLS], BF16, name="wb_woven1", align_bytes=64)[:],
-            h4[1][:, (PACK - 1) * HALF :].bitcast(BF16),
-            h_woven[1][:, : PACK * WB_COLS],
+        h4 = [
+            keep.tile([P, PACK * HALF], F32, name="h4_0", align_bytes=64)[:],
+            shared.tile([P, PACK * HALF], F32, name="h4_1", align_bytes=64, offset=0)[:],
         ]
-        shared_planes = keep.tile([P, HALF], U8, name="shared_planes", align_bytes=64)
+        h_woven = [keep.tile([P, PACK * HALF], BF16, name=f"h_woven{h}", align_bytes=64)[:] for h in range(HALVES)]
+        wb_woven = [h_woven[1][:, (c % 2) * PACK * WB_COLS : (c % 2 + 1) * PACK * WB_COLS] for c in range(4)]
 
-        def scale_ranks(h, t):
+        def scale_ranks(h, t, c0, width):
             nc.vector.tensor_tensor(
-                out=h4[h][:, t * HALF : (t + 1) * HALF],
-                in0=g_win[t][:].indirect(half_list(h)),
-                in1=a_sb[h, t][:],
+                out=h4[h][:, t * HALF + c0 : t * HALF + c0 + width],
+                in0=g_win[t][:].indirect(part_list(h * HALF + c0, width)),
+                in1=a_sb[h, t][:, c0 : c0 + width],
                 op=MULT,
             )
 
-        def weave_h(h):
-            nc.vector.tensor_copy(
-                out=h_woven[h].rearrange("p (c i t) -> p c t i", i=LINE, t=PACK),
-                in_=h4[h].rearrange("p (t c i) -> p c t i", t=PACK, i=LINE),
+        def weave_h(h, q, weave):
+            c0 = q * QUARTER
+            weave(
+                out=h_woven[h][:, PACK * c0 : PACK * (c0 + QUARTER)].rearrange(
+                    "p (c i t) -> p c t i", i=LINE, t=PACK
+                ),
+                in_=h4[h]
+                .rearrange("p (t c) -> p t c", t=PACK)[:, :, c0 : c0 + QUARTER]
+                .rearrange("p t (c i) -> p c t i", i=LINE),
             )
 
         def quantise_h(h):
             codes = keep.tile([P, HALF], U32, name=f"h_codes{h}", align_bytes=64)[:]
-            if h == 0:
-                plane = shared_planes[4:P, :]
-            else:
-                plane = w4_codes[1][:, (AHEAD - 2) * 2 * P : AHEAD * 2 * P]
+            plane = keep.tile([P, HALF], U8, name=f"h_plane{h}", align_bytes=64)[:]
             nc.vector.quantize_mx(out=codes.bitcast(FP8X4), scales=plane, in_=h_woven[h])
             return codes, plane
 
-        def quantise_wb(c):
-            weave = nc.vector.tensor_copy if c == WB_PIECES - 1 else nc.scalar.copy
+        def weave_wb(c, weave):
             weave(
                 out=wb_woven[c].rearrange("p (c i j) -> p c j i", i=LINE, j=PACK),
-                in_=wb_raw[c][1].rearrange("p j (c i) -> p c j i", i=LINE),
+                in_=wb_raw[c].rearrange("p j (c i) -> p c j i", i=LINE),
             )
-            codes = keep.tile([P, WB_COLS], U32, name=f"wb_codes{c}", align_bytes=64)
-            if c == 0:
-                plane = shared_planes[:, :WB_COLS]
-            else:
-                plane = keep.tile([P, WB_COLS], U8, name=f"wb_plane{c}", align_bytes=64)[:]
-            nc.vector.quantize_mx(out=codes[:].bitcast(FP8X4), scales=plane, in_=wb_woven[c])
-            return codes, plane
 
-        for t in range(PACK - 1):
-            for h in range(HALVES):
-                scale_ranks(h, t)
-        scale_ranks(0, PACK - 1)
-        weave_h(0)
-        wb_mx = [quantise_wb(0)]
-        h_mx = [quantise_h(0)]
-        wb_mx.extend([quantise_wb(c) for c in range(1, WB_PIECES)])
+        def quantise_wb(c):
+            codes = keep.tile([P, WB_COLS], U32, name=f"wb_codes{c}", align_bytes=64)[:]
+            plane = keep.tile([P, WB_COLS], U8, name=f"wb_plane{c}", align_bytes=64)[:]
+            nc.vector.quantize_mx(out=codes.bitcast(FP8X4), scales=plane, in_=wb_woven[c])
+            return codes, plane
 
         v_scales = [v_planes, v_plane1]
         y_banks = {}
 
-        def base_passes(h, n):
+        def base_pass(h, n, a):
             cols = slice(h * HALF, (h + 1) * HALF)
-            y_banks[h, n] = psum.tile([P, HALF], F32, name=f"y_bank{h}_{n}", tag=f"bank{n}")
-            for a in range(PASSES):
-                nc.tensor.matmul_mx(
-                    out=y_banks[h, n][:],
-                    lhsT=w4_codes[a][:, 2 * n * P : 2 * (n + 1) * P].bitcast(FP4X4),
-                    lhsT_scale=w4_planes[:, a, n * P : (n + 1) * P],
-                    rhs=v_codes[a][:, cols].bitcast(FP8X4),
-                    rhs_scale=v_scales[a][:, cols],
-                    start=(a == 0),
-                    stop=False,
-                )
+            if a == 0:
+                b = HALVES * n + h if n < EARLY else REUSE[h, n]
+                y_banks[h, n] = psum.tile([P, HALF], F32, name=f"y_bank{h}_{n}", tag=f"bank{b}")
+            if n < W4_FIRST:
+                codes = w4_early[a][:, 2 * n * P : 2 * (n + 1) * P]
+            else:
+                codes = w4_late[:, a, 2 * (n - W4_FIRST) * P : 2 * (n - W4_FIRST + 1) * P]
+            nc.tensor.matmul_mx(
+                out=y_banks[h, n][:],
+                lhsT=codes.bitcast(FP4X4),
+                lhsT_scale=w4_planes[:, a, n * P : (n + 1) * P],
+                rhs=v_codes[a][:, cols].bitcast(FP8X4),
+                rhs_scale=v_scales[a][:, cols],
+                start=(a == 0),
+                stop=False,
+            )
 
         def close(h, n):
-            bank = y_banks[h, n]
             c, m0 = divmod(n * P, WB_COLS)
             nc.tensor.matmul_mx(
-                out=bank[:],
+                out=y_banks[h, n][:],
                 lhsT=wb_mx[c][0][:, m0 : m0 + P].bitcast(FP8X4),
                 lhsT_scale=wb_mx[c][1][:, m0 : m0 + P],
                 rhs=h_mx[h][0].bitcast(FP8X4),
@@ -263,26 +261,71 @@ def tile_list_tenant_rank_scales_kernel(
                 start=False,
                 stop=True,
             )
-            if h == 0 and n < PACK:
-                result = wb_raw[WB_PIECES - 2][0][:, n * HALF : (n + 1) * HALF]
+
+        def empty(h, n, result, on_vector):
+            if on_vector:
+                nc.vector.tensor_scalar_add(out=result, in0=y_banks[h, n][:], scalar1=bo_cols[:, n : n + 1])
             else:
-                result = keep.tile([P, HALF], F32, name=f"result{h}_{n}")[:]
-            if (h == 1 and n % 2 == 0) or (h == 0 and n == N_TILES - 1):
-                nc.vector.tensor_scalar_add(out=result, in0=bank[:], scalar1=bo_cols[:, n : n + 1])
-            else:
-                nc.scalar.activation(out=result, in_=bank[:], func=IDENTITY, bias=bo_cols[:, n : n + 1])
+                nc.scalar.activation(out=result, in_=y_banks[h, n][:], func=IDENTITY, bias=bo_cols[:, n : n + 1])
+
+        def finish_half(h, n, result, on_vector):
+            close(h, n)
+            empty(h, n, result, on_vector)
             nc.sync.dma_start(out=out[n * P : (n + 1) * P, h * HALF : (h + 1) * HALF], in_=result)
 
-        for n in range(N_TILES):
-            base_passes(0, n)
-        for n in range(N_TILES):
-            close(0, n)
-        for n in range(AHEAD):
-            base_passes(1, n)
-        scale_ranks(1, PACK - 1)
-        weave_h(1)
+        def new_result(h, n):
+            return keep.tile([P, HALF], F32, name=f"result{h}_{n}")[:]
+
+        for a in range(PASSES):
+            for h in range(HALVES):
+                for n in range(EARLY):
+                    base_pass(h, n, a)
+
+        for t in range(PACK - 1):
+            for h in range(HALVES):
+                scale_ranks(h, t, 0, HALF)
+        last = PACK - 1
+        scale_ranks(0, last, 0, QUARTER)
+        weave_h(0, 0, nc.scalar.copy)
+        scale_ranks(0, last, QUARTER, QUARTER)
+        weave_h(0, 1, nc.vector.tensor_copy)
+        h_mx = [quantise_h(0)]
+        scale_ranks(1, last, 0, QUARTER)
+        scale_ranks(1, last, QUARTER, QUARTER)
+        weave_wb(0, nc.scalar.copy)
+        wb_mx = [quantise_wb(0)]
+        weave_wb(1, nc.scalar.copy)
+        weave_h(1, 0, nc.vector.tensor_copy)
+        wb_mx.append(quantise_wb(1))
+        weave_h(1, 1, nc.vector.tensor_copy)
         h_mx.append(quantise_h(1))
-        for n in range(N_TILES):
-            if n >= AHEAD:
-                base_passes(1, n)
-            close(1, n)
+        w4_late = shared.tile([P, PASSES, 2 * (N - W4_FIRST * P)], U8, name="w4_late", align_bytes=64, offset=0)
+        nc.sync.dma_start(
+            out=w4_late[:].bitcast(I32),
+            in_=w4_words[:, :, 2 * W4_FIRST * P :].rearrange("a p c -> p a c").bitcast(I32),
+        )
+        for n in range(EARLY):
+            result = wb_loads[1][0][:, n * HALF : (n + 1) * HALF] if n < 2 else new_result(0, n)
+            finish_half(0, n, result, False)
+        res1 = [new_result(1, n) for n in range(EARLY)]
+        for n in range(EARLY):
+            finish_half(1, n, res1[n], n == EARLY - 1)
+
+        for c in range(2, 4):
+            weave_wb(c, nc.vector.tensor_copy)
+        for c in range(2, 4):
+            wb_mx.append(quantise_wb(c))
+
+        for n in range(EARLY, N_TILES):
+            for h in range(HALVES):
+                for a in range(PASSES):
+                    base_pass(h, n, a)
+            if n < N_TILES - 1:
+                result = keep.tile([P, S], F32, name=f"result{n}")
+                for h in range(HALVES):
+                    close(h, n)
+                    empty(h, n, result[:, h * HALF : (h + 1) * HALF], h == 0)
+                nc.sync.dma_start(out=out[n * P : (n + 1) * P, :], in_=result[:])
+            else:
+                for h in range(HALVES):
+                    finish_half(h, n, new_result(h, n), h == 0)

@@ -37,6 +37,7 @@ SHIFT_ROWS = 112
 
 
 WA_SCALAR = (96, 56)
+LATE_SLOT = 2
 REUSE = {(h, n): HALVES * ((2 * (n - EARLY) + h) % EARLY) + (2 * (n - EARLY) + h) // EARLY for n in range(EARLY, N_TILES) for h in range(HALVES)}
 
 
@@ -128,8 +129,9 @@ def tile_list_tenant_rank_scales_kernel(
             )
         w4_early = [load_w4_early(0)]
         g_win.extend([load_g(t) for t in range(2, PACK)])
+        wb_loads = [load_wb("wb_raw0", 0, WB_COLS)]
         w4_early.append(load_w4_early(1))
-        wb_loads = [load_wb(f"wb_raw{c}", c * WB_COLS, WB_COLS) for c in range(2)]
+        wb_loads.append(load_wb("wb_raw1", WB_COLS, WB_COLS))
         wb_late = load_wb("wb_late", EARLY_COLS, N - EARLY_COLS)[1]
         wb_raw = [wb_loads[0][1], wb_loads[1][1], wb_late[:, :, :WB_COLS], wb_late[:, :, WB_COLS:]]
 
@@ -145,7 +147,8 @@ def tile_list_tenant_rank_scales_kernel(
             src = wa_raw[a][:].rearrange("p j (m t) -> p m j t", t=PACK)
             cut = WA_SCALAR[a]
             nc.scalar.copy(out=dst[:, :cut], in_=src[:, :cut])
-            nc.vector.tensor_copy(out=dst[:, cut:], in_=src[:, cut:])
+            if cut < P:
+                nc.vector.tensor_copy(out=dst[:, cut:], in_=src[:, cut:])
             codes = keep.tile([P, R], U32, name=f"wa_codes{a}", align_bytes=64)
             plane = keep.tile([P, R], U8, name=f"wa_plane{a}", align_bytes=64)
             nc.vector.quantize_mx(out=codes[:].bitcast(FP8X4), scales=plane[:], in_=woven[:])
@@ -162,11 +165,14 @@ def tile_list_tenant_rank_scales_kernel(
 
         a_sb = {}
         a_banks = {}
-        for a in range(PASSES):
-            for t in range(PACK):
-                for h in range(HALVES):
+        early = [(h, t) for t in range(PACK) for h in range(HALVES) if h == 0 or t < LATE_SLOT]
+        late = [(1, t) for t in range(LATE_SLOT, PACK)]
+        for banks in (early, late):
+            for step in range(PASSES):
+                for h, t in banks:
+                    a = PASSES - 1 - step if (h == 1 and t >= LATE_SLOT) else step
                     cols = slice(h * HALF, (h + 1) * HALF)
-                    if a == 0:
+                    if step == 0:
                         a_banks[h, t] = psum.tile([P, HALF], F32, name=f"a_bank{h}_{t}", tag=f"bank{HALVES * t + h}")
                     bank = a_banks[h, t]
                     nc.tensor.matmul_mx(
@@ -175,10 +181,10 @@ def tile_list_tenant_rank_scales_kernel(
                         lhsT_scale=wa_planes[a][:, t * P : (t + 1) * P],
                         rhs=v_codes[a][:, cols].bitcast(FP8X4),
                         rhs_scale=v_planes[4 * a : P, cols],
-                        start=(a == 0),
-                        stop=(a == PASSES - 1),
+                        start=(step == 0),
+                        stop=(step == PASSES - 1),
                     )
-                    if a == PASSES - 1:
+                    if step == PASSES - 1:
                         a_sb[h, t] = keep.tile([P, HALF], F32, name=f"a_sb{h}_{t}")
                         nc.scalar.activation(
                             out=a_sb[h, t][:], in_=bank[:], func=IDENTITY, bias=ba_cols[:, t : t + 1]
@@ -276,10 +282,9 @@ def tile_list_tenant_rank_scales_kernel(
         def new_result(h, n):
             return keep.tile([P, HALF], F32, name=f"result{h}_{n}")[:]
 
-        for a in range(PASSES):
-            for h in range(HALVES):
-                for n in range(EARLY):
-                    base_pass(h, n, a)
+        for h, a in ((0, 0), (1, 0), (0, 1)):
+            for n in range(EARLY):
+                base_pass(h, n, a)
 
         for t in range(PACK - 1):
             for h in range(HALVES):
@@ -307,15 +312,16 @@ def tile_list_tenant_rank_scales_kernel(
         for n in range(EARLY):
             result = wb_loads[1][0][:, n * HALF : (n + 1) * HALF] if n < 2 else new_result(0, n)
             finish_half(0, n, result, False)
+            if n == 1:
+                for m in range(EARLY):
+                    base_pass(1, m, 1)
         res1 = [new_result(1, n) for n in range(EARLY)]
         for n in range(EARLY):
             finish_half(1, n, res1[n], n == EARLY - 1)
-
         for c in range(2, 4):
             weave_wb(c, nc.vector.tensor_copy)
         for c in range(2, 4):
             wb_mx.append(quantise_wb(c))
-
         for n in range(EARLY, N_TILES):
             for h in range(HALVES):
                 for a in range(PASSES):

@@ -32,7 +32,7 @@ QUARTER = HALF // 2
 WB_COLS = 256
 EARLY = N_TILES // 2
 EARLY_COLS = EARLY * P
-W4_FIRST = EARLY + 1
+W4_FIRST = EARLY
 SHIFT_ROWS = 112
 
 
@@ -129,9 +129,13 @@ def tile_list_tenant_rank_scales_kernel(
             )
         w4_early = [load_w4_early(0)]
         g_win.extend([load_g(t) for t in range(2, PACK)])
-        wb_loads = [load_wb("wb_raw0", 0, WB_COLS)]
         w4_early.append(load_w4_early(1))
-        wb_loads.append(load_wb("wb_raw1", WB_COLS, WB_COLS))
+        wb_loads = [load_wb(f"wb_raw{c}", c * WB_COLS, WB_COLS) for c in range(2)]
+        w4_late = keep.tile([P, PASSES, 2 * (N - W4_FIRST * P)], U8, name="w4_late", align_bytes=64)
+        nc.sync.dma_start(
+            out=w4_late[:].bitcast(I32),
+            in_=w4_words[:, :, 2 * W4_FIRST * P :].rearrange("a p c -> p a c").bitcast(I32),
+        )
         wb_late = load_wb("wb_late", EARLY_COLS, N - EARLY_COLS)[1]
         wb_raw = [wb_loads[0][1], wb_loads[1][1], wb_late[:, :, :WB_COLS], wb_late[:, :, WB_COLS:]]
 
@@ -191,11 +195,21 @@ def tile_list_tenant_rank_scales_kernel(
                         )
 
         h4 = [
-            keep.tile([P, PACK * HALF], F32, name="h4_0", align_bytes=64)[:],
-            shared.tile([P, PACK * HALF], F32, name="h4_1", align_bytes=64, offset=0)[:],
+            shared.tile([P, PACK * HALF], F32, name="h4_0", align_bytes=64, offset=0)[:],
+            keep.tile([P, PACK * HALF], F32, name="h4_1", align_bytes=64)[:],
         ]
-        h_woven = [keep.tile([P, PACK * HALF], BF16, name=f"h_woven{h}", align_bytes=64)[:] for h in range(HALVES)]
-        wb_woven = [h_woven[1][:, (c % 2) * PACK * WB_COLS : (c % 2 + 1) * PACK * WB_COLS] for c in range(4)]
+        h_woven = [
+            keep.tile([P, PACK * HALF], BF16, name="h_woven0", align_bytes=64)[:],
+            shared.tile([P, PACK * HALF], BF16, name="h_woven1", align_bytes=64, offset=0)[:],
+        ]
+        wb_woven = [keep.tile([P, PACK * WB_COLS], BF16, name=f"wb_woven{c}", align_bytes=64)[:] for c in range(4)]
+        h_mx = [
+            (
+                keep.tile([P, HALF], U32, name=f"h_codes{h}", align_bytes=64)[:],
+                keep.tile([P, HALF], U8, name=f"h_plane{h}", align_bytes=64)[:],
+            )
+            for h in range(HALVES)
+        ]
 
         def scale_ranks(h, t, c0, width):
             nc.vector.tensor_tensor(
@@ -216,11 +230,13 @@ def tile_list_tenant_rank_scales_kernel(
                 .rearrange("p t (c i) -> p c t i", i=LINE),
             )
 
-        def quantise_h(h):
-            codes = keep.tile([P, HALF], U32, name=f"h_codes{h}", align_bytes=64)[:]
-            plane = keep.tile([P, HALF], U8, name=f"h_plane{h}", align_bytes=64)[:]
-            nc.vector.quantize_mx(out=codes.bitcast(FP8X4), scales=plane, in_=h_woven[h])
-            return codes, plane
+        def quantise_h(h, q):
+            cols = slice(q * QUARTER, (q + 1) * QUARTER)
+            nc.vector.quantize_mx(
+                out=h_mx[h][0][:, cols].bitcast(FP8X4),
+                scales=h_mx[h][1][:, cols],
+                in_=h_woven[h][:, PACK * q * QUARTER : PACK * (q + 1) * QUARTER],
+            )
 
         def weave_wb(c, weave):
             weave(
@@ -282,7 +298,7 @@ def tile_list_tenant_rank_scales_kernel(
         def new_result(h, n):
             return keep.tile([P, HALF], F32, name=f"result{h}_{n}")[:]
 
-        for h, a in ((0, 0), (1, 0), (0, 1)):
+        for h, a in ((0, 0), (1, 0), (0, 1), (1, 1)):
             for n in range(EARLY):
                 base_pass(h, n, a)
 
@@ -290,31 +306,23 @@ def tile_list_tenant_rank_scales_kernel(
             for h in range(HALVES):
                 scale_ranks(h, t, 0, HALF)
         last = PACK - 1
-        scale_ranks(0, last, 0, QUARTER)
-        weave_h(0, 0, nc.scalar.copy)
-        scale_ranks(0, last, QUARTER, QUARTER)
-        weave_h(0, 1, nc.vector.tensor_copy)
-        h_mx = [quantise_h(0)]
-        scale_ranks(1, last, 0, QUARTER)
-        scale_ranks(1, last, QUARTER, QUARTER)
-        weave_wb(0, nc.scalar.copy)
+        for q in range(2):
+            scale_ranks(0, last, q * QUARTER, QUARTER)
+            weave_h(0, q, nc.scalar.copy)
+        scale_ranks(1, last, 0, HALF)
+        weave_wb(0, nc.vector.tensor_copy)
+        for q in range(2):
+            quantise_h(0, q)
         wb_mx = [quantise_wb(0)]
         weave_wb(1, nc.scalar.copy)
-        weave_h(1, 0, nc.vector.tensor_copy)
+        for q in range(2):
+            weave_h(1, q, nc.vector.tensor_copy)
         wb_mx.append(quantise_wb(1))
-        weave_h(1, 1, nc.vector.tensor_copy)
-        h_mx.append(quantise_h(1))
-        w4_late = shared.tile([P, PASSES, 2 * (N - W4_FIRST * P)], U8, name="w4_late", align_bytes=64, offset=0)
-        nc.sync.dma_start(
-            out=w4_late[:].bitcast(I32),
-            in_=w4_words[:, :, 2 * W4_FIRST * P :].rearrange("a p c -> p a c").bitcast(I32),
-        )
+        for q in range(2):
+            quantise_h(1, q)
         for n in range(EARLY):
             result = wb_loads[1][0][:, n * HALF : (n + 1) * HALF] if n < 2 else new_result(0, n)
             finish_half(0, n, result, False)
-            if n == 1:
-                for m in range(EARLY):
-                    base_pass(1, m, 1)
         res1 = [new_result(1, n) for n in range(EARLY)]
         for n in range(EARLY):
             finish_half(1, n, res1[n], n == EARLY - 1)

@@ -37,6 +37,8 @@ SHIFT_ROWS = 112
 
 
 WA_SCALAR = (96, 56)
+WB0_AT = PACK * HALF - QUARTER
+WB0_STEP = 3 * WB_COLS
 LATE_SLOT = 2
 REUSE = {(h, n): HALVES * ((2 * (n - EARLY) + h) % EARLY) + (2 * (n - EARLY) + h) // EARLY for n in range(EARLY, N_TILES) for h in range(HALVES)}
 
@@ -55,7 +57,8 @@ def tile_list_tenant_rank_scales_kernel(
 
         tab_planes = keep.tile([P, T], U8, name="tab_planes", align_bytes=64)
         nc.vector.memset(tab_planes[:].bitcast(I32), 0)
-        ba_cols = keep.tile([P, PACK], F32, name="ba_cols")
+        ba_row = keep.tile([P, R], F32, name="ba_row")
+        nc.vector.memset(ba_row[:], 0.0)
         bo_rows = keep.tile([P, P], F32, name="bo_rows")
         nc.vector.memset(bo_rows[:], 0.0)
         ident = keep.tile([P, P], F32, name="ident")
@@ -108,9 +111,9 @@ def tile_list_tenant_rank_scales_kernel(
                 in_=tab_scales[:, 4 * q : 4 * q + 4, :].bitcast(I32),
             )
         nc.sync.dma_start(out=bo_rows[0:N_TILES, :], in_=bo.rearrange("(c p) -> c p", p=P))
+        nc.sync.dma_start(out=ba_row[0:1, :], in_=ba.rearrange("(o r) -> o r", o=1))
         wa_raw = [load_wa(a) for a in range(PASSES)]
         tab_win.append(load_table(1))
-        nc.sync.dma_start(out=ba_cols[:], in_=ba.rearrange("(p t) -> p t", t=PACK))
 
         v_codes = [keep.tile([P, S], U32, name=f"v_codes{a}", align_bytes=64) for a in range(PASSES)]
         v_planes = keep.tile([P, S], U8, name="v_planes", align_bytes=64)
@@ -130,19 +133,30 @@ def tile_list_tenant_rank_scales_kernel(
         w4_early = [load_w4_early(0)]
         g_win.extend([load_g(t) for t in range(2, PACK)])
         w4_early.append(load_w4_early(1))
-        wb_loads = [load_wb(f"wb_raw{c}", c * WB_COLS, WB_COLS) for c in range(2)]
+        common = keep.tile([P, WB0_AT + PACK * WB0_STEP], F32, name="common", align_bytes=64)
+        wb_raw0 = common[:, WB0_AT:].rearrange("p (j n) -> p j n", j=PACK)[:, :, :WB_COLS]
+        nc.sync.dma_start(out=wb_raw0, in_=wb_rows[:, :, :WB_COLS])
+        second = keep.tile([P, HALF - P + PACK * WB_COLS], F32, name="second")
+        wb_raw1 = second[:, HALF - P :].rearrange("p (j n) -> p j n", j=PACK)
+        nc.sync.dma_start(out=wb_raw1, in_=wb_rows[:, :, WB_COLS : 2 * WB_COLS])
         w4_late = keep.tile([P, PASSES, 2 * (N - W4_FIRST * P)], U8, name="w4_late", align_bytes=64)
         nc.sync.dma_start(
             out=w4_late[:].bitcast(I32),
             in_=w4_words[:, :, 2 * W4_FIRST * P :].rearrange("a p c -> p a c").bitcast(I32),
         )
         wb_late = load_wb("wb_late", EARLY_COLS, N - EARLY_COLS)[1]
-        wb_raw = [wb_loads[0][1], wb_loads[1][1], wb_late[:, :, :WB_COLS], wb_late[:, :, WB_COLS:]]
+        wb_raw = [wb_raw0, wb_raw1, wb_late[:, :, :WB_COLS], wb_late[:, :, WB_COLS:]]
 
         bo_bank = psum.tile([P, P], F32, name="bo_bank", tag=f"bank{N_TILES - 1}")
         nc.tensor.transpose(bo_bank[:], bo_rows[:], ident[:])
         bo_cols = keep.tile([P, N_TILES], F32, name="bo_cols")
         nc.scalar.activation(out=bo_cols[:], in_=bo_bank[:, 0:N_TILES], func=IDENTITY)
+
+        ba_bank = psum.tile([P, PACK, P], F32, name="ba_bank", tag=f"bank{N_TILES - 2}")
+        for t in range(PACK):
+            nc.tensor.transpose(ba_bank[:, t, :], ba_row[:, t:R:PACK], ident[:])
+        ba_cols = keep.tile([P, PACK], F32, name="ba_cols")
+        nc.scalar.activation(out=ba_cols[:], in_=ba_bank[:, :, 0], func=IDENTITY)
 
         wa_codes, wa_planes = [], []
         for a in range(PASSES):
@@ -194,15 +208,17 @@ def tile_list_tenant_rank_scales_kernel(
                             out=a_sb[h, t][:], in_=bank[:], func=IDENTITY, bias=ba_cols[:, t : t + 1]
                         )
 
-        h4 = [
-            shared.tile([P, PACK * HALF], F32, name="h4_0", align_bytes=64, offset=0)[:],
-            keep.tile([P, PACK * HALF], F32, name="h4_1", align_bytes=64)[:],
-        ]
-        h_woven = [
-            keep.tile([P, PACK * HALF], BF16, name="h_woven0", align_bytes=64)[:],
-            shared.tile([P, PACK * HALF], BF16, name="h_woven1", align_bytes=64, offset=0)[:],
-        ]
-        wb_woven = [keep.tile([P, PACK * WB_COLS], BF16, name=f"wb_woven{c}", align_bytes=64)[:] for c in range(4)]
+        h4 = [keep.tile([P, PACK * HALF], F32, name="h4_0", align_bytes=64)[:], common[:, : PACK * HALF]]
+        h_woven = {
+            (h, q): keep.tile([P, PACK * QUARTER], BF16, name=f"h_woven{h}_{q}", align_bytes=64)[:]
+            for h, q in ((0, 0), (0, 1), (1, 1))
+        }
+        row1 = WB0_AT + WB0_STEP
+        h_woven[1, 0] = common[:, row1 : row1 + 2 * WB_COLS].bitcast(BF16)
+        wb_woven = {
+            c: keep.tile([P, PACK * WB_COLS], BF16, name=f"wb_woven{c}", align_bytes=64)[:] for c in (0, 2, 3)
+        }
+        wb_woven[1] = common[:, row1 + 2 * WB_COLS : row1 + 4 * WB_COLS].bitcast(BF16)
         h_mx = [
             (
                 keep.tile([P, HALF], U32, name=f"h_codes{h}", align_bytes=64)[:],
@@ -222,7 +238,7 @@ def tile_list_tenant_rank_scales_kernel(
         def weave_h(h, q, weave):
             c0 = q * QUARTER
             weave(
-                out=h_woven[h][:, PACK * c0 : PACK * (c0 + QUARTER)].rearrange(
+                out=h_woven[h, q].rearrange(
                     "p (c i t) -> p c t i", i=LINE, t=PACK
                 ),
                 in_=h4[h]
@@ -235,13 +251,13 @@ def tile_list_tenant_rank_scales_kernel(
             nc.vector.quantize_mx(
                 out=h_mx[h][0][:, cols].bitcast(FP8X4),
                 scales=h_mx[h][1][:, cols],
-                in_=h_woven[h][:, PACK * q * QUARTER : PACK * (q + 1) * QUARTER],
+                in_=h_woven[h, q],
             )
 
-        def weave_wb(c, weave):
+        def weave_wb(c, weave, c0=0, width=WB_COLS):
             weave(
-                out=wb_woven[c].rearrange("p (c i j) -> p c j i", i=LINE, j=PACK),
-                in_=wb_raw[c].rearrange("p j (c i) -> p c j i", i=LINE),
+                out=wb_woven[c][:, PACK * c0 : PACK * (c0 + width)].rearrange("p (c i j) -> p c j i", i=LINE, j=PACK),
+                in_=wb_raw[c][:, :, c0 : c0 + width].rearrange("p j (c i) -> p c j i", i=LINE),
             )
 
         def quantise_wb(c):
@@ -306,22 +322,25 @@ def tile_list_tenant_rank_scales_kernel(
             for h in range(HALVES):
                 scale_ranks(h, t, 0, HALF)
         last = PACK - 1
-        for q in range(2):
-            scale_ranks(0, last, q * QUARTER, QUARTER)
-            weave_h(0, q, nc.scalar.copy)
-        scale_ranks(1, last, 0, HALF)
-        weave_wb(0, nc.vector.tensor_copy)
+        scale_ranks(0, last, 0, QUARTER)
+        weave_h(0, 0, nc.scalar.copy)
+        scale_ranks(0, last, QUARTER, QUARTER)
+        scale_ranks(1, last, 0, QUARTER)
+        weave_h(0, 1, nc.vector.tensor_copy)
+        weave_wb(0, nc.scalar.copy)
         for q in range(2):
             quantise_h(0, q)
         wb_mx = [quantise_wb(0)]
-        weave_wb(1, nc.scalar.copy)
-        for q in range(2):
-            weave_h(1, q, nc.vector.tensor_copy)
+        scale_ranks(1, last, QUARTER, QUARTER)
+        weave_wb(1, nc.scalar.copy, 0, P)
+        weave_wb(1, nc.vector.tensor_copy, P, P)
+        weave_h(1, 0, nc.vector.tensor_copy)
         wb_mx.append(quantise_wb(1))
+        weave_h(1, 1, nc.vector.tensor_copy)
         for q in range(2):
             quantise_h(1, q)
         for n in range(EARLY):
-            result = wb_loads[1][0][:, n * HALF : (n + 1) * HALF] if n < 2 else new_result(0, n)
+            result = second[:, :HALF] if n == 0 else new_result(0, n)
             finish_half(0, n, result, False)
         res1 = [new_result(1, n) for n in range(EARLY)]
         for n in range(EARLY):

@@ -33,7 +33,7 @@ WB_COLS = 256
 EARLY = N_TILES // 2
 EARLY_COLS = EARLY * P
 W4_FIRST = EARLY
-SHIFT_ROWS = 112
+SHIFT = QUADRANT // PASSES
 
 
 WA_SCALAR = (96, 56)
@@ -55,7 +55,7 @@ def tile_list_tenant_rank_scales_kernel(
         offsets = keep.tile([P, S // LIST_ROWS], U16, name="offsets")
         nc.sync.dma_start(offsets[:], offs)
 
-        tab_planes = keep.tile([P, T], U8, name="tab_planes", align_bytes=64)
+        tab_planes = shared.tile([P, T], U8, name="tab_planes", align_bytes=64, offset=0)
         nc.vector.memset(tab_planes[:].bitcast(I32), 0)
         ba_row = keep.tile([P, R], F32, name="ba_row")
         nc.vector.memset(ba_row[:], 0.0)
@@ -87,7 +87,7 @@ def tile_list_tenant_rank_scales_kernel(
         g_rows = gT.rearrange("(p t) c -> t p c", t=PACK)
 
         def load_g(t):
-            win = keep.tile([P, T], F32, name=f"g_win{t}", align_bytes=64)
+            win = shared.tile([P, T], F32, name=f"g_win{t}", align_bytes=64, offset=4 * T * t)
             nc.sync.dma_start(out=win[:], in_=g_rows[t])
             return win
 
@@ -105,10 +105,10 @@ def tile_list_tenant_rank_scales_kernel(
             return flat, raw
 
         tab_win = [load_table(0)]
-        for q in range(P // QUADRANT):
+        for r in range(4):
             nc.sync.dma_start(
-                out=tab_planes[QUADRANT * q : QUADRANT * q + PASSES * 4, :].bitcast(I32),
-                in_=tab_scales[:, 4 * q : 4 * q + 4, :].bitcast(I32),
+                out=tab_planes[r:P:SHIFT, :].bitcast(I32),
+                in_=tab_scales[:, r:SCALE_ROWS:4, :].rearrange("a q c -> q a c").bitcast(I32),
             )
         nc.sync.dma_start(out=bo_rows[0:N_TILES, :], in_=bo.rearrange("(c p) -> c p", p=P))
         nc.sync.dma_start(out=ba_row[0:1, :], in_=ba.rearrange("(o r) -> o r", o=1))
@@ -120,11 +120,9 @@ def tile_list_tenant_rank_scales_kernel(
         nc.vector.tensor_copy(out=v_codes[0][:], in_=tab_win[0][:].indirect(offsets[:]))
         nc.vector.tensor_copy(out=v_planes[:], in_=tab_planes[:].indirect(offsets[:]))
 
+        nc.sync.dma_start(out=v_plane1[0 : P - SHIFT, :].bitcast(I32), in_=v_planes[SHIFT:P, :].bitcast(I32))
+        v_scales = [v_planes, v_plane1]
         g_win = [load_g(t) for t in range(2)]
-        nc.sync.dma_start(
-            out=v_plane1[0:SHIFT_ROWS, :].bitcast(I32),
-            in_=v_planes[4 : 4 + SHIFT_ROWS, :].bitcast(I32),
-        )
         for r in range(4):
             nc.sync.dma_start(
                 out=w4_planes[r:P:QUADRANT, :, :].bitcast(I32),
@@ -198,7 +196,7 @@ def tile_list_tenant_rank_scales_kernel(
                         lhsT=wa_codes[a][:, t * P : (t + 1) * P].bitcast(FP8X4),
                         lhsT_scale=wa_planes[a][:, t * P : (t + 1) * P],
                         rhs=v_codes[a][:, cols].bitcast(FP8X4),
-                        rhs_scale=v_planes[4 * a : P, cols],
+                        rhs_scale=v_scales[a][:, cols],
                         start=(step == 0),
                         stop=(step == PASSES - 1),
                     )
@@ -266,7 +264,6 @@ def tile_list_tenant_rank_scales_kernel(
             nc.vector.quantize_mx(out=codes.bitcast(FP8X4), scales=plane, in_=wb_woven[c])
             return codes, plane
 
-        v_scales = [v_planes, v_plane1]
         y_banks = {}
 
         def base_pass(h, n, a):
@@ -342,14 +339,14 @@ def tile_list_tenant_rank_scales_kernel(
         for n in range(EARLY):
             result = second[:, :HALF] if n == 0 else new_result(0, n)
             finish_half(0, n, result, False)
-        res1 = [new_result(1, n) for n in range(EARLY)]
-        for n in range(EARLY):
-            finish_half(1, n, res1[n], n == EARLY - 1)
         for c in range(2, 4):
             weave_wb(c, nc.vector.tensor_copy)
-        for c in range(2, 4):
-            wb_mx.append(quantise_wb(c))
+        wb_mx.append(quantise_wb(2))
+        for n in range(EARLY):
+            finish_half(1, n, new_result(1, n), n == EARLY - 1)
         for n in range(EARLY, N_TILES):
+            if n == EARLY + 1:
+                wb_mx.append(quantise_wb(3))
             for h in range(HALVES):
                 for a in range(PASSES):
                     base_pass(h, n, a)

@@ -33,13 +33,14 @@ WB_COLS = 256
 EARLY = N_TILES // 2
 EARLY_COLS = EARLY * P
 W4_FIRST = EARLY
+G_AT = T // 2
 SHIFT = QUADRANT // PASSES
 
 
-WA_SCALAR = (96, 56)
-WB0_AT = PACK * HALF - QUARTER
-WB0_STEP = 3 * WB_COLS
-LATE_SLOT = 2
+WA_SCALAR = (80, 80)
+WB0_STEP = 2 * WB_COLS
+WB1_AT = PACK * HALF - P
+WB1_STEP = HALF + P
 REUSE = {(h, n): HALVES * ((2 * (n - EARLY) + h) % EARLY) + (2 * (n - EARLY) + h) // EARLY for n in range(EARLY, N_TILES) for h in range(HALVES)}
 
 
@@ -87,7 +88,7 @@ def tile_list_tenant_rank_scales_kernel(
         g_rows = gT.rearrange("(p t) c -> t p c", t=PACK)
 
         def load_g(t):
-            win = shared.tile([P, T], F32, name=f"g_win{t}", align_bytes=64, offset=4 * T * t)
+            win = shared.tile([P, T], F32, name=f"g_win{t}", align_bytes=64, offset=G_AT + 4 * T * t)
             nc.sync.dma_start(out=win[:], in_=g_rows[t])
             return win
 
@@ -104,38 +105,38 @@ def tile_list_tenant_rank_scales_kernel(
             nc.sync.dma_start(out=raw, in_=wb_rows[:, :, c0 : c0 + width])
             return flat, raw
 
-        tab_win = [load_table(0)]
+        wa_raw = [load_wa(0)]
         for r in range(4):
             nc.sync.dma_start(
                 out=tab_planes[r:P:SHIFT, :].bitcast(I32),
                 in_=tab_scales[:, r:SCALE_ROWS:4, :].rearrange("a q c -> q a c").bitcast(I32),
             )
-        nc.sync.dma_start(out=bo_rows[0:N_TILES, :], in_=bo.rearrange("(c p) -> c p", p=P))
         nc.sync.dma_start(out=ba_row[0:1, :], in_=ba.rearrange("(o r) -> o r", o=1))
-        wa_raw = [load_wa(a) for a in range(PASSES)]
+        nc.sync.dma_start(out=bo_rows[0:N_TILES, :], in_=bo.rearrange("(c p) -> c p", p=P))
+        wa_raw.append(load_wa(1))
+        tab_win = [load_table(0)]
         tab_win.append(load_table(1))
 
         v_codes = [keep.tile([P, S], U32, name=f"v_codes{a}", align_bytes=64) for a in range(PASSES)]
         v_planes = keep.tile([P, S], U8, name="v_planes", align_bytes=64)
-        nc.vector.tensor_copy(out=v_codes[0][:], in_=tab_win[0][:].indirect(offsets[:]))
         nc.vector.tensor_copy(out=v_planes[:], in_=tab_planes[:].indirect(offsets[:]))
 
         nc.sync.dma_start(out=v_plane1[0 : P - SHIFT, :].bitcast(I32), in_=v_planes[SHIFT:P, :].bitcast(I32))
         v_scales = [v_planes, v_plane1]
-        g_win = [load_g(t) for t in range(2)]
+        g_win = [load_g(t) for t in range(PACK - 1)]
         for r in range(4):
             nc.sync.dma_start(
                 out=w4_planes[r:P:QUADRANT, :, :].bitcast(I32),
                 in_=w4_scales[:, r:SCALE_ROWS:4, :].rearrange("a q c -> q a c").bitcast(I32),
             )
         w4_early = [load_w4_early(0)]
-        g_win.extend([load_g(t) for t in range(2, PACK)])
+        g_win.append(load_g(PACK - 1))
         w4_early.append(load_w4_early(1))
-        common = keep.tile([P, WB0_AT + PACK * WB0_STEP], F32, name="common", align_bytes=64)
-        wb_raw0 = common[:, WB0_AT:].rearrange("p (j n) -> p j n", j=PACK)[:, :, :WB_COLS]
+        first = keep.tile([P, PACK * WB0_STEP], F32, name="first", align_bytes=64)
+        wb_raw0 = first[:].rearrange("p (j n) -> p j n", j=PACK)[:, :, :WB_COLS]
         nc.sync.dma_start(out=wb_raw0, in_=wb_rows[:, :, :WB_COLS])
-        second = keep.tile([P, HALF - P + PACK * WB_COLS], F32, name="second")
-        wb_raw1 = second[:, HALF - P :].rearrange("p (j n) -> p j n", j=PACK)
+        common = keep.tile([P, WB1_AT + PACK * WB1_STEP], F32, name="common", align_bytes=64)
+        wb_raw1 = common[:, WB1_AT:].rearrange("p (j n) -> p j n", j=PACK)[:, :, :WB_COLS]
         nc.sync.dma_start(out=wb_raw1, in_=wb_rows[:, :, WB_COLS : 2 * WB_COLS])
         w4_late = keep.tile([P, PASSES, 2 * (N - W4_FIRST * P)], U8, name="w4_late", align_bytes=64)
         nc.sync.dma_start(
@@ -144,11 +145,6 @@ def tile_list_tenant_rank_scales_kernel(
         )
         wb_late = load_wb("wb_late", EARLY_COLS, N - EARLY_COLS)[1]
         wb_raw = [wb_raw0, wb_raw1, wb_late[:, :, :WB_COLS], wb_late[:, :, WB_COLS:]]
-
-        bo_bank = psum.tile([P, P], F32, name="bo_bank", tag=f"bank{N_TILES - 1}")
-        nc.tensor.transpose(bo_bank[:], bo_rows[:], ident[:])
-        bo_cols = keep.tile([P, N_TILES], F32, name="bo_cols")
-        nc.scalar.activation(out=bo_cols[:], in_=bo_bank[:, 0:N_TILES], func=IDENTITY)
 
         ba_bank = psum.tile([P, PACK, P], F32, name="ba_bank", tag=f"bank{N_TILES - 2}")
         for t in range(PACK):
@@ -166,63 +162,76 @@ def tile_list_tenant_rank_scales_kernel(
             if cut < P:
                 nc.vector.tensor_copy(out=dst[:, cut:], in_=src[:, cut:])
             codes = keep.tile([P, R], U32, name=f"wa_codes{a}", align_bytes=64)
-            plane = keep.tile([P, R], U8, name=f"wa_plane{a}", align_bytes=64)
+            if a == 0:
+                plane = shared.tile([P, R], U8, name="wa_plane0", align_bytes=64, offset=0)
+            else:
+                plane = keep.tile([P, R], U8, name="wa_plane1", align_bytes=64)
             nc.vector.quantize_mx(out=codes[:].bitcast(FP8X4), scales=plane[:], in_=woven[:])
             wa_codes.append(codes)
             wa_planes.append(plane)
 
+        bo_bank = psum.tile([P, P], F32, name="bo_bank", tag=f"bank{N_TILES - 1}")
+        nc.tensor.transpose(bo_bank[:], bo_rows[:], ident[:])
+        bo_cols = keep.tile([P, N_TILES], F32, name="bo_cols")
+        nc.scalar.activation(out=bo_cols[:], in_=bo_bank[:, 0:N_TILES], func=IDENTITY)
+
         def part_list(c0, width):
             return offsets[:, c0 // LIST_ROWS : (c0 + width) // LIST_ROWS]
 
-        for h in range(HALVES):
-            nc.vector.tensor_copy(
-                out=v_codes[1][:, h * HALF : (h + 1) * HALF], in_=tab_win[1][:].indirect(part_list(h * HALF, HALF))
-            )
+        for a in range(PASSES):
+            for h in range(HALVES):
+                nc.vector.tensor_copy(
+                    out=v_codes[a][:, h * HALF : (h + 1) * HALF], in_=tab_win[a][:].indirect(part_list(h * HALF, HALF))
+                )
 
-        a_sb = {}
+        a_sb = {
+            (h, t): keep.tile([P, HALF], F32, name=f"a_sb{h}_{t}") for t in range(PACK) for h in range(HALVES)
+        }
+        sums = [(0, 0, 0, QUARTER, 0), (0, 0, QUARTER, QUARTER, N_TILES - 1)]
+        sums.extend((h, t, 0, HALF, HALVES * t + h) for t in range(PACK) for h in range(HALVES) if (h, t) != (0, 0))
         a_banks = {}
-        early = [(h, t) for t in range(PACK) for h in range(HALVES) if h == 0 or t < LATE_SLOT]
-        late = [(1, t) for t in range(LATE_SLOT, PACK)]
-        for banks in (early, late):
-            for step in range(PASSES):
-                for h, t in banks:
-                    a = PASSES - 1 - step if (h == 1 and t >= LATE_SLOT) else step
-                    cols = slice(h * HALF, (h + 1) * HALF)
-                    if step == 0:
-                        a_banks[h, t] = psum.tile([P, HALF], F32, name=f"a_bank{h}_{t}", tag=f"bank{HALVES * t + h}")
-                    bank = a_banks[h, t]
-                    nc.tensor.matmul_mx(
-                        out=bank[:],
-                        lhsT=wa_codes[a][:, t * P : (t + 1) * P].bitcast(FP8X4),
-                        lhsT_scale=wa_planes[a][:, t * P : (t + 1) * P],
-                        rhs=v_codes[a][:, cols].bitcast(FP8X4),
-                        rhs_scale=v_scales[a][:, cols],
-                        start=(step == 0),
-                        stop=(step == PASSES - 1),
-                    )
-                    if step == PASSES - 1:
-                        a_sb[h, t] = keep.tile([P, HALF], F32, name=f"a_sb{h}_{t}")
-                        nc.scalar.activation(
-                            out=a_sb[h, t][:], in_=bank[:], func=IDENTITY, bias=ba_cols[:, t : t + 1]
-                        )
+
+        def first_product(h, t, c0, width, b, a):
+            cols = slice(h * HALF + c0, h * HALF + c0 + width)
+            opens = (h, t, c0) not in a_banks
+            if opens:
+                a_banks[h, t, c0] = psum.tile([P, HALF], F32, name=f"a_bank{h}_{t}_{c0}", tag=f"bank{b}")
+            bank = a_banks[h, t, c0][:, :width]
+            nc.tensor.matmul_mx(
+                out=bank,
+                lhsT=wa_codes[a][:, t * P : (t + 1) * P].bitcast(FP8X4),
+                lhsT_scale=wa_planes[a][:, t * P : (t + 1) * P],
+                rhs=v_codes[a][:, cols].bitcast(FP8X4),
+                rhs_scale=v_scales[a][:, cols],
+                start=opens,
+                stop=not opens,
+            )
+            if not opens:
+                nc.scalar.activation(
+                    out=a_sb[h, t][:, c0 : c0 + width], in_=bank, func=IDENTITY, bias=ba_cols[:, t : t + 1]
+                )
+
+        opened_early = [entry for entry in sums if entry[0] == 0] + [entry for entry in sums if entry[:2] == (1, 0)]
+        for entry in opened_early:
+            first_product(*entry, 0)
+        for entry in sums:
+            first_product(*entry, 1)
+            if entry not in opened_early:
+                first_product(*entry, 0)
 
         h4 = [keep.tile([P, PACK * HALF], F32, name="h4_0", align_bytes=64)[:], common[:, : PACK * HALF]]
-        h_woven = {
-            (h, q): keep.tile([P, PACK * QUARTER], BF16, name=f"h_woven{h}_{q}", align_bytes=64)[:]
-            for h, q in ((0, 0), (0, 1), (1, 1))
-        }
-        row1 = WB0_AT + WB0_STEP
-        h_woven[1, 0] = common[:, row1 : row1 + 2 * WB_COLS].bitcast(BF16)
+        h_woven = [keep.tile([P, PACK * HALF], BF16, name=f"h_woven{h}", align_bytes=64)[:] for h in range(HALVES)]
         wb_woven = {
             c: keep.tile([P, PACK * WB_COLS], BF16, name=f"wb_woven{c}", align_bytes=64)[:] for c in (0, 2, 3)
         }
-        wb_woven[1] = common[:, row1 + 2 * WB_COLS : row1 + 4 * WB_COLS].bitcast(BF16)
+        wb_woven[1] = first[:, : 2 * WB_COLS].bitcast(BF16)
+        packed = keep.tile([P, HALF], U8, name="packed", align_bytes=64)
         h_mx = [
             (
-                keep.tile([P, HALF], U32, name=f"h_codes{h}", align_bytes=64)[:],
-                keep.tile([P, HALF], U8, name=f"h_plane{h}", align_bytes=64)[:],
-            )
-            for h in range(HALVES)
+                keep.tile([P, HALF], U32, name="h_codes0", align_bytes=64)[:],
+                keep.tile([P, HALF], U8, name="h_plane0", align_bytes=64)[:],
+            ),
+            (keep.tile([P, HALF], U32, name="h_codes1", align_bytes=64)[:], packed[4:P, :]),
         ]
 
         def scale_ranks(h, t, c0, width):
@@ -233,15 +242,14 @@ def tile_list_tenant_rank_scales_kernel(
                 op=MULT,
             )
 
-        def weave_h(h, q, weave):
-            c0 = q * QUARTER
+        def weave_h(h, u, c0, width, weave):
             weave(
-                out=h_woven[h, q].rearrange(
-                    "p (c i t) -> p c t i", i=LINE, t=PACK
-                ),
+                out=h_woven[h][:, PACK * c0 : PACK * (c0 + width)].rearrange(
+                    "p (c i u e) -> p u c e i", i=LINE, u=2, e=2
+                )[:, u],
                 in_=h4[h]
-                .rearrange("p (t c) -> p t c", t=PACK)[:, :, c0 : c0 + QUARTER]
-                .rearrange("p t (c i) -> p c t i", i=LINE),
+                .rearrange("p (t c) -> p t c", t=PACK)[:, 2 * u : 2 * u + 2, c0 : c0 + width]
+                .rearrange("p e (c i) -> p c e i", i=LINE),
             )
 
         def quantise_h(h, q):
@@ -249,7 +257,7 @@ def tile_list_tenant_rank_scales_kernel(
             nc.vector.quantize_mx(
                 out=h_mx[h][0][:, cols].bitcast(FP8X4),
                 scales=h_mx[h][1][:, cols],
-                in_=h_woven[h, q],
+                in_=h_woven[h][:, PACK * q * QUARTER : PACK * (q + 1) * QUARTER],
             )
 
         def weave_wb(c, weave, c0=0, width=WB_COLS):
@@ -260,7 +268,10 @@ def tile_list_tenant_rank_scales_kernel(
 
         def quantise_wb(c):
             codes = keep.tile([P, WB_COLS], U32, name=f"wb_codes{c}", align_bytes=64)[:]
-            plane = keep.tile([P, WB_COLS], U8, name=f"wb_plane{c}", align_bytes=64)[:]
+            if c == 1:
+                plane = packed[:, :WB_COLS]
+            else:
+                plane = keep.tile([P, WB_COLS], U8, name=f"wb_plane{c}", align_bytes=64)[:]
             nc.vector.quantize_mx(out=codes.bitcast(FP8X4), scales=plane, in_=wb_woven[c])
             return codes, plane
 
@@ -317,28 +328,36 @@ def tile_list_tenant_rank_scales_kernel(
 
         for t in range(PACK - 1):
             for h in range(HALVES):
-                scale_ranks(h, t, 0, HALF)
+                if (h, t) == (0, 0):
+                    for q in range(2):
+                        scale_ranks(h, t, q * QUARTER, QUARTER)
+                else:
+                    scale_ranks(h, t, 0, HALF)
+                if t == 1:
+                    weave_h(h, 0, 0, HALF, nc.scalar.copy)
         last = PACK - 1
         scale_ranks(0, last, 0, QUARTER)
-        weave_h(0, 0, nc.scalar.copy)
+        weave_h(0, 1, 0, QUARTER, nc.scalar.copy)
         scale_ranks(0, last, QUARTER, QUARTER)
         scale_ranks(1, last, 0, QUARTER)
-        weave_h(0, 1, nc.vector.tensor_copy)
+        weave_h(0, 1, QUARTER, QUARTER, nc.vector.tensor_copy)
+        weave_h(1, 1, 0, QUARTER, nc.vector.tensor_copy)
         weave_wb(0, nc.scalar.copy)
         for q in range(2):
             quantise_h(0, q)
         wb_mx = [quantise_wb(0)]
-        scale_ranks(1, last, QUARTER, QUARTER)
         weave_wb(1, nc.scalar.copy, 0, P)
         weave_wb(1, nc.vector.tensor_copy, P, P)
-        weave_h(1, 0, nc.vector.tensor_copy)
+        first_result = WB1_AT + WB1_STEP + P - HALF
+        finish_half(0, 0, common[:, first_result : first_result + HALF], False)
+        finish_half(0, 1, new_result(0, 1), False)
+        scale_ranks(1, last, QUARTER, QUARTER)
         wb_mx.append(quantise_wb(1))
-        weave_h(1, 1, nc.vector.tensor_copy)
+        weave_h(1, 1, QUARTER, QUARTER, nc.vector.tensor_copy)
+        for n in range(2, EARLY):
+            finish_half(0, n, new_result(0, n), False)
         for q in range(2):
             quantise_h(1, q)
-        for n in range(EARLY):
-            result = second[:, :HALF] if n == 0 else new_result(0, n)
-            finish_half(0, n, result, False)
         for c in range(2, 4):
             weave_wb(c, nc.vector.tensor_copy)
         wb_mx.append(quantise_wb(2))

@@ -37,7 +37,7 @@ G_AT = T // 2
 SHIFT = QUADRANT // PASSES
 
 
-WA_SCALAR = (80, 80)
+WA_SCALAR = (80, 68)
 WB0_STEP = 2 * WB_COLS
 WB1_AT = PACK * HALF - P
 WB1_STEP = HALF + P
@@ -54,10 +54,9 @@ def tile_list_tenant_rank_scales_kernel(
         psum = ctx.enter_context(tc.psum_pool(name="psum", bufs=1))
 
         offsets = keep.tile([P, S // LIST_ROWS], U16, name="offsets")
-        nc.sync.dma_start(offsets[:], offs)
 
         tab_planes = shared.tile([P, T], U8, name="tab_planes", align_bytes=64, offset=0)
-        nc.vector.memset(tab_planes[:].bitcast(I32), 0)
+        nc.gpsimd.memset(tab_planes[:].bitcast(I32), 0)
         ba_row = keep.tile([P, R], F32, name="ba_row")
         nc.vector.memset(ba_row[:], 0.0)
         bo_rows = keep.tile([P, P], F32, name="bo_rows")
@@ -77,13 +76,11 @@ def tile_list_tenant_rank_scales_kernel(
             )
             return win
 
-        def load_wa(a):
-            raw = keep.tile([P, PACK, R], F32, name=f"wa_raw{a}")
-            nc.sync.dma_start(
-                out=raw[:],
-                in_=wa[a * K_PASS : (a + 1) * K_PASS, :].rearrange("(p j) r -> p j r", j=PACK),
-            )
-            return raw
+        wa_raw = [keep.tile([P, PACK, R], F32, name=f"wa_raw{a}") for a in range(PASSES)]
+
+        def load_wa(a, j0, j1):
+            rows = wa[a * K_PASS : (a + 1) * K_PASS, :].rearrange("(p j) r -> p j r", j=PACK)
+            nc.sync.dma_start(out=wa_raw[a][:, j0:j1, :], in_=rows[:, j0:j1, :])
 
         g_rows = gT.rearrange("(p t) c -> t p c", t=PACK)
 
@@ -105,16 +102,18 @@ def tile_list_tenant_rank_scales_kernel(
             nc.sync.dma_start(out=raw, in_=wb_rows[:, :, c0 : c0 + width])
             return flat, raw
 
-        wa_raw = [load_wa(0)]
+        nc.sync.dma_start(offsets[:], offs)
+        load_wa(0, 0, 2)
         for r in range(4):
             nc.sync.dma_start(
                 out=tab_planes[r:P:SHIFT, :].bitcast(I32),
                 in_=tab_scales[:, r:SCALE_ROWS:4, :].rearrange("a q c -> q a c").bitcast(I32),
             )
+        load_wa(0, 2, PACK)
+        tab_win = [load_table(0)]
         nc.sync.dma_start(out=ba_row[0:1, :], in_=ba.rearrange("(o r) -> o r", o=1))
         nc.sync.dma_start(out=bo_rows[0:N_TILES, :], in_=bo.rearrange("(c p) -> c p", p=P))
-        wa_raw.append(load_wa(1))
-        tab_win = [load_table(0)]
+        load_wa(1, 0, PACK)
         tab_win.append(load_table(1))
 
         v_codes = [keep.tile([P, S], U32, name=f"v_codes{a}", align_bytes=64) for a in range(PASSES)]
@@ -178,17 +177,15 @@ def tile_list_tenant_rank_scales_kernel(
         def part_list(c0, width):
             return offsets[:, c0 // LIST_ROWS : (c0 + width) // LIST_ROWS]
 
-        for a in range(PASSES):
-            for h in range(HALVES):
-                nc.vector.tensor_copy(
-                    out=v_codes[a][:, h * HALF : (h + 1) * HALF], in_=tab_win[a][:].indirect(part_list(h * HALF, HALF))
-                )
+        for a, cuts in enumerate(((0, HALF, S), range(0, S + 1, QUARTER))):
+            for c0, c1 in zip(cuts, cuts[1:]):
+                nc.vector.tensor_copy(out=v_codes[a][:, c0:c1], in_=tab_win[a][:].indirect(part_list(c0, c1 - c0)))
 
         a_sb = {
             (h, t): keep.tile([P, HALF], F32, name=f"a_sb{h}_{t}") for t in range(PACK) for h in range(HALVES)
         }
-        sums = [(0, 0, 0, QUARTER, 0), (0, 0, QUARTER, QUARTER, N_TILES - 1)]
-        sums.extend((h, t, 0, HALF, HALVES * t + h) for t in range(PACK) for h in range(HALVES) if (h, t) != (0, 0))
+        sums = [(h, 0, q * QUARTER, QUARTER, N_TILES - 1 - h if q else h) for h in range(HALVES) for q in range(2)]
+        sums.extend((h, t, 0, HALF, HALVES * t + h) for t in range(1, PACK) for h in range(HALVES))
         a_banks = {}
 
         def first_product(h, t, c0, width, b, a):
@@ -211,7 +208,7 @@ def tile_list_tenant_rank_scales_kernel(
                     out=a_sb[h, t][:, c0 : c0 + width], in_=bank, func=IDENTITY, bias=ba_cols[:, t : t + 1]
                 )
 
-        opened_early = [entry for entry in sums if entry[0] == 0] + [entry for entry in sums if entry[:2] == (1, 0)]
+        opened_early = sums[:7]
         for entry in opened_early:
             first_product(*entry, 0)
         for entry in sums:
@@ -328,7 +325,7 @@ def tile_list_tenant_rank_scales_kernel(
 
         for t in range(PACK - 1):
             for h in range(HALVES):
-                if (h, t) == (0, 0):
+                if t == 0:
                     for q in range(2):
                         scale_ranks(h, t, q * QUARTER, QUARTER)
                 else:

@@ -38,9 +38,7 @@ SHIFT = QUADRANT // PASSES
 
 
 WA_SCALAR = (80, 68)
-WB0_STEP = 2 * WB_COLS
-WB1_AT = PACK * HALF - P
-WB1_STEP = HALF + P
+WB_AT = (PACK - 1) * HALF
 REUSE = {(h, n): HALVES * ((2 * (n - EARLY) + h) % EARLY) + (2 * (n - EARLY) + h) // EARLY for n in range(EARLY, N_TILES) for h in range(HALVES)}
 
 
@@ -131,11 +129,10 @@ def tile_list_tenant_rank_scales_kernel(
         w4_early = [load_w4_early(0)]
         g_win.append(load_g(PACK - 1))
         w4_early.append(load_w4_early(1))
-        first = keep.tile([P, PACK * WB0_STEP], F32, name="first", align_bytes=64)
-        wb_raw0 = first[:].rearrange("p (j n) -> p j n", j=PACK)[:, :, :WB_COLS]
+        common = keep.tile([P, WB_AT + PACK * EARLY_COLS], F32, name="common", align_bytes=64)
+        wb_early = common[:, WB_AT:].rearrange("p (j n) -> p j n", j=PACK)
+        wb_raw0, wb_raw1 = wb_early[:, :, :WB_COLS], wb_early[:, :, WB_COLS:]
         nc.sync.dma_start(out=wb_raw0, in_=wb_rows[:, :, :WB_COLS])
-        common = keep.tile([P, WB1_AT + PACK * WB1_STEP], F32, name="common", align_bytes=64)
-        wb_raw1 = common[:, WB1_AT:].rearrange("p (j n) -> p j n", j=PACK)[:, :, :WB_COLS]
         nc.sync.dma_start(out=wb_raw1, in_=wb_rows[:, :, WB_COLS : 2 * WB_COLS])
         w4_late = keep.tile([P, PASSES, 2 * (N - W4_FIRST * P)], U8, name="w4_late", align_bytes=64)
         nc.sync.dma_start(
@@ -219,16 +216,14 @@ def tile_list_tenant_rank_scales_kernel(
         h4 = [keep.tile([P, PACK * HALF], F32, name="h4_0", align_bytes=64)[:], common[:, : PACK * HALF]]
         h_woven = [keep.tile([P, PACK * HALF], BF16, name=f"h_woven{h}", align_bytes=64)[:] for h in range(HALVES)]
         wb_woven = {
-            c: keep.tile([P, PACK * WB_COLS], BF16, name=f"wb_woven{c}", align_bytes=64)[:] for c in (0, 2, 3)
+            c: keep.tile([P, PACK * WB_COLS], BF16, name=f"wb_woven{c}", align_bytes=64)[:] for c in range(N // WB_COLS)
         }
-        wb_woven[1] = first[:, : 2 * WB_COLS].bitcast(BF16)
-        packed = keep.tile([P, HALF], U8, name="packed", align_bytes=64)
         h_mx = [
             (
-                keep.tile([P, HALF], U32, name="h_codes0", align_bytes=64)[:],
-                keep.tile([P, HALF], U8, name="h_plane0", align_bytes=64)[:],
-            ),
-            (keep.tile([P, HALF], U32, name="h_codes1", align_bytes=64)[:], packed[4:P, :]),
+                keep.tile([P, HALF], U32, name=f"h_codes{h}", align_bytes=64)[:],
+                keep.tile([P, HALF], U8, name=f"h_plane{h}", align_bytes=64)[:],
+            )
+            for h in range(HALVES)
         ]
 
         def scale_ranks(h, t, c0, width):
@@ -265,10 +260,7 @@ def tile_list_tenant_rank_scales_kernel(
 
         def quantise_wb(c):
             codes = keep.tile([P, WB_COLS], U32, name=f"wb_codes{c}", align_bytes=64)[:]
-            if c == 1:
-                plane = packed[:, :WB_COLS]
-            else:
-                plane = keep.tile([P, WB_COLS], U8, name=f"wb_plane{c}", align_bytes=64)[:]
+            plane = keep.tile([P, WB_COLS], U8, name=f"wb_plane{c}", align_bytes=64)[:]
             nc.vector.quantize_mx(out=codes.bitcast(FP8X4), scales=plane, in_=wb_woven[c])
             return codes, plane
 
@@ -333,40 +325,40 @@ def tile_list_tenant_rank_scales_kernel(
                 if t == 1:
                     weave_h(h, 0, 0, HALF, nc.scalar.copy)
         last = PACK - 1
-        scale_ranks(0, last, 0, QUARTER)
-        weave_h(0, 1, 0, QUARTER, nc.scalar.copy)
-        scale_ranks(0, last, QUARTER, QUARTER)
-        scale_ranks(1, last, 0, QUARTER)
-        weave_h(0, 1, QUARTER, QUARTER, nc.vector.tensor_copy)
-        weave_h(1, 1, 0, QUARTER, nc.vector.tensor_copy)
-        weave_wb(0, nc.scalar.copy)
+        for q in range(2):
+            scale_ranks(0, last, q * QUARTER, QUARTER)
+        for q in range(2):
+            weave_h(0, 1, q * QUARTER, QUARTER, nc.vector.tensor_copy)
+        for c in range(2):
+            weave_wb(c, nc.scalar.copy)
         for q in range(2):
             quantise_h(0, q)
         wb_mx = [quantise_wb(0)]
-        weave_wb(1, nc.scalar.copy, 0, P)
-        weave_wb(1, nc.vector.tensor_copy, P, P)
-        first_result = WB1_AT + WB1_STEP + P - HALF
-        finish_half(0, 0, common[:, first_result : first_result + HALF], False)
-        finish_half(0, 1, new_result(0, 1), False)
-        scale_ranks(1, last, QUARTER, QUARTER)
+        scale_ranks(1, last, 0, QUARTER)
         wb_mx.append(quantise_wb(1))
-        weave_h(1, 1, QUARTER, QUARTER, nc.vector.tensor_copy)
-        for n in range(2, EARLY):
+        first_result = WB_AT + EARLY_COLS + WB_COLS
+        finish_half(0, 0, common[:, first_result : first_result + HALF], False)
+        for n in range(1, EARLY):
             finish_half(0, n, new_result(0, n), False)
+        for c0 in (QUARTER, QUARTER + P):
+            scale_ranks(1, last, c0, P)
+        weave_h(1, 1, 0, HALF - P, nc.vector.tensor_copy)
+        weave_h(1, 1, HALF - P, P, nc.vector.tensor_copy)
         for q in range(2):
             quantise_h(1, q)
-        for c in range(2, 4):
-            weave_wb(c, nc.vector.tensor_copy)
+        weave_wb(2, nc.vector.tensor_copy)
+        weave_wb(3, nc.vector.tensor_copy, 0, P)
         wb_mx.append(quantise_wb(2))
+        weave_wb(3, nc.vector.tensor_copy, P, P)
         for n in range(EARLY):
             finish_half(1, n, new_result(1, n), n == EARLY - 1)
         for n in range(EARLY, N_TILES):
             if n == EARLY + 1:
                 wb_mx.append(quantise_wb(3))
-            for h in range(HALVES):
-                for a in range(PASSES):
-                    base_pass(h, n, a)
             if n < N_TILES - 1:
+                for h in range(HALVES):
+                    for a in range(PASSES):
+                        base_pass(h, n, a)
                 result = keep.tile([P, S], F32, name=f"result{n}")
                 for h in range(HALVES):
                     close(h, n)
@@ -374,4 +366,6 @@ def tile_list_tenant_rank_scales_kernel(
                 nc.sync.dma_start(out=out[n * P : (n + 1) * P, :], in_=result[:])
             else:
                 for h in range(HALVES):
+                    for a in range(PASSES):
+                        base_pass(h, n, a)
                     finish_half(h, n, new_result(h, n), h == 0)

@@ -38,7 +38,7 @@ SHIFT = QUADRANT // PASSES
 
 
 WA_SCALAR = (80, 68)
-WB_AT = (PACK - 1) * HALF
+WB_AT = PACK * S - HALF
 REUSE = {(h, n): HALVES * ((2 * (n - EARLY) + h) % EARLY) + (2 * (n - EARLY) + h) // EARLY for n in range(EARLY, N_TILES) for h in range(HALVES)}
 
 
@@ -174,13 +174,11 @@ def tile_list_tenant_rank_scales_kernel(
         def part_list(c0, width):
             return offsets[:, c0 // LIST_ROWS : (c0 + width) // LIST_ROWS]
 
-        for a, cuts in enumerate(((0, HALF, S), range(0, S + 1, QUARTER))):
+        for a, cuts in enumerate(((0, S), range(0, S + 1, QUARTER))):
             for c0, c1 in zip(cuts, cuts[1:]):
                 nc.vector.tensor_copy(out=v_codes[a][:, c0:c1], in_=tab_win[a][:].indirect(part_list(c0, c1 - c0)))
 
-        a_sb = {
-            (h, t): keep.tile([P, HALF], F32, name=f"a_sb{h}_{t}") for t in range(PACK) for h in range(HALVES)
-        }
+        a_sb = [keep.tile([P, S], F32, name=f"a_sb{t}") for t in range(PACK)]
         sums = [(h, 0, q * QUARTER, QUARTER, N_TILES - 1 - h if q else h) for h in range(HALVES) for q in range(2)]
         sums.extend((h, t, 0, HALF, HALVES * t + h) for t in range(1, PACK) for h in range(HALVES))
         a_banks = {}
@@ -201,9 +199,7 @@ def tile_list_tenant_rank_scales_kernel(
                 stop=not opens,
             )
             if not opens:
-                nc.scalar.activation(
-                    out=a_sb[h, t][:, c0 : c0 + width], in_=bank, func=IDENTITY, bias=ba_cols[:, t : t + 1]
-                )
+                nc.scalar.activation(out=a_sb[t][:, cols], in_=bank, func=IDENTITY, bias=ba_cols[:, t : t + 1])
 
         opened_early = sums[:7]
         for entry in opened_early:
@@ -213,7 +209,7 @@ def tile_list_tenant_rank_scales_kernel(
             if entry not in opened_early:
                 first_product(*entry, 0)
 
-        h4 = [keep.tile([P, PACK * HALF], F32, name="h4_0", align_bytes=64)[:], common[:, : PACK * HALF]]
+        h4 = common[:, : PACK * S].rearrange("p (t c) -> p t c", t=PACK)
         h_woven = [keep.tile([P, PACK * HALF], BF16, name=f"h_woven{h}", align_bytes=64)[:] for h in range(HALVES)]
         wb_woven = {
             c: keep.tile([P, PACK * WB_COLS], BF16, name=f"wb_woven{c}", align_bytes=64)[:] for c in range(N // WB_COLS)
@@ -228,9 +224,9 @@ def tile_list_tenant_rank_scales_kernel(
 
         def scale_ranks(h, t, c0, width):
             nc.vector.tensor_tensor(
-                out=h4[h][:, t * HALF + c0 : t * HALF + c0 + width],
+                out=h4[:, t, h * HALF + c0 : h * HALF + c0 + width],
                 in0=g_win[t][:].indirect(part_list(h * HALF + c0, width)),
-                in1=a_sb[h, t][:, c0 : c0 + width],
+                in1=a_sb[t][:, h * HALF + c0 : h * HALF + c0 + width],
                 op=MULT,
             )
 
@@ -239,9 +235,9 @@ def tile_list_tenant_rank_scales_kernel(
                 out=h_woven[h][:, PACK * c0 : PACK * (c0 + width)].rearrange(
                     "p (c i u e) -> p u c e i", i=LINE, u=2, e=2
                 )[:, u],
-                in_=h4[h]
-                .rearrange("p (t c) -> p t c", t=PACK)[:, 2 * u : 2 * u + 2, c0 : c0 + width]
-                .rearrange("p e (c i) -> p c e i", i=LINE),
+                in_=h4[:, 2 * u : 2 * u + 2, h * HALF + c0 : h * HALF + c0 + width].rearrange(
+                    "p e (c i) -> p c e i", i=LINE
+                ),
             )
 
         def quantise_h(h, q):
@@ -261,7 +257,13 @@ def tile_list_tenant_rank_scales_kernel(
         def quantise_wb(c):
             codes = keep.tile([P, WB_COLS], U32, name=f"wb_codes{c}", align_bytes=64)[:]
             plane = keep.tile([P, WB_COLS], U8, name=f"wb_plane{c}", align_bytes=64)[:]
-            nc.vector.quantize_mx(out=codes.bitcast(FP8X4), scales=plane, in_=wb_woven[c])
+            width = P if c == 0 else WB_COLS
+            for c0 in range(0, WB_COLS, width):
+                nc.vector.quantize_mx(
+                    out=codes[:, c0 : c0 + width].bitcast(FP8X4),
+                    scales=plane[:, c0 : c0 + width],
+                    in_=wb_woven[c][:, PACK * c0 : PACK * (c0 + width)],
+                )
             return codes, plane
 
         y_banks = {}
@@ -315,15 +317,13 @@ def tile_list_tenant_rank_scales_kernel(
             for n in range(EARLY):
                 base_pass(h, n, a)
 
-        for t in range(PACK - 1):
-            for h in range(HALVES):
-                if t == 0:
-                    for q in range(2):
-                        scale_ranks(h, t, q * QUARTER, QUARTER)
-                else:
-                    scale_ranks(h, t, 0, HALF)
-                if t == 1:
-                    weave_h(h, 0, 0, HALF, nc.scalar.copy)
+        for q in range(2):
+            scale_ranks(0, 0, q * QUARTER, QUARTER)
+        scale_ranks(1, 0, 0, HALF)
+        for h in range(HALVES):
+            scale_ranks(h, 1, 0, HALF)
+            weave_h(h, 0, 0, HALF, nc.scalar.copy)
+        scale_ranks(0, 2, 0, S)
         last = PACK - 1
         for q in range(2):
             scale_ranks(0, last, q * QUARTER, QUARTER)

@@ -100,8 +100,8 @@ def tile_list_tenant_rank_scales_kernel(
             nc.sync.dma_start(out=raw, in_=wb_rows[:, :, c0 : c0 + width])
             return flat, raw
 
-        nc.sync.dma_start(offsets[:], offs)
         load_wa(0, 0, 2)
+        nc.sync.dma_start(offsets[:], offs)
         for r in range(4):
             nc.sync.dma_start(
                 out=tab_planes[r:P:SHIFT, :].bitcast(I32),
@@ -257,7 +257,7 @@ def tile_list_tenant_rank_scales_kernel(
         def quantise_wb(c):
             codes = keep.tile([P, WB_COLS], U32, name=f"wb_codes{c}", align_bytes=64)[:]
             plane = keep.tile([P, WB_COLS], U8, name=f"wb_plane{c}", align_bytes=64)[:]
-            width = P if c == 0 else WB_COLS
+            width = P if c < 2 else WB_COLS
             for c0 in range(0, WB_COLS, width):
                 nc.vector.quantize_mx(
                     out=codes[:, c0 : c0 + width].bitcast(FP8X4),

@@ -34,7 +34,7 @@ EARLY = N_TILES // 2
 EARLY_COLS = EARLY * P
 W4_FIRST = EARLY
 G_AT = T // 2
-SHIFT = QUADRANT // PASSES
+SPREAD = P // (PASSES * SCALE_ROWS)
 
 
 WA_SCALAR = (80, 68)
@@ -61,8 +61,8 @@ def tile_list_tenant_rank_scales_kernel(
         nc.vector.memset(bo_rows[:], 0.0)
         ident = keep.tile([P, P], F32, name="ident")
         make_identity(nc, ident[:])
-        v_plane1 = keep.tile([P, S], U8, name="v_plane1", align_bytes=64)
-        nc.vector.memset(v_plane1[:].bitcast(I32), 0)
+        v_planes = keep.tile([P, PASSES, S], U8, name="v_planes", align_bytes=64)
+        nc.vector.memset(v_planes[:].bitcast(I32), 0)
         w4_planes = keep.tile([P, PASSES, N], U8, name="w4_planes", align_bytes=64)
         nc.vector.memset(w4_planes[:].bitcast(I32), 0)
 
@@ -102,24 +102,27 @@ def tile_list_tenant_rank_scales_kernel(
 
         load_wa(0, 0, 2)
         nc.sync.dma_start(offsets[:], offs)
-        for r in range(4):
-            nc.sync.dma_start(
-                out=tab_planes[r:P:SHIFT, :].bitcast(I32),
-                in_=tab_scales[:, r:SCALE_ROWS:4, :].rearrange("a q c -> q a c").bitcast(I32),
-            )
+        nc.sync.dma_start(
+            out=tab_planes[0:P:SPREAD, :].bitcast(I32),
+            in_=tab_scales.rearrange("a q c -> q a c").bitcast(I32),
+        )
         load_wa(0, 2, PACK)
         tab_win = [load_table(0)]
         nc.sync.dma_start(out=ba_row[0:1, :], in_=ba.rearrange("(o r) -> o r", o=1))
         nc.sync.dma_start(out=bo_rows[0:N_TILES, :], in_=bo.rearrange("(c p) -> c p", p=P))
         load_wa(1, 0, PACK)
-        tab_win.append(load_table(1))
 
         v_codes = [keep.tile([P, S], U32, name=f"v_codes{a}", align_bytes=64) for a in range(PASSES)]
-        v_planes = keep.tile([P, S], U8, name="v_planes", align_bytes=64)
-        nc.vector.tensor_copy(out=v_planes[:], in_=tab_planes[:].indirect(offsets[:]))
-
-        nc.sync.dma_start(out=v_plane1[0 : P - SHIFT, :].bitcast(I32), in_=v_planes[SHIFT:P, :].bitcast(I32))
-        v_scales = [v_planes, v_plane1]
+        picked = keep.tile([P, S], U8, name="picked", align_bytes=64)
+        nc.vector.tensor_copy(out=picked[:], in_=tab_planes[:].indirect(offsets[:]))
+        for quad in (0, 2, 1, 3):
+            p0 = quad * QUADRANT
+            nc.sync.dma_start(
+                out=v_planes[p0 : p0 + 4, :, :].bitcast(I32),
+                in_=picked[p0 : p0 + QUADRANT : SPREAD, :].bitcast(I32),
+            )
+        tab_win.append(load_table(1))
+        v_scales = [v_planes[:, a, :] for a in range(PASSES)]
         g_win = [load_g(t) for t in range(PACK - 1)]
         for r in range(4):
             nc.sync.dma_start(

@@ -34,6 +34,7 @@ EARLY = N_TILES // 2
 EARLY_COLS = EARLY * P
 W4_FIRST = EARLY
 G_AT = T // 2
+WB_SCALAR = 192
 SPREAD = P // (PASSES * SCALE_ROWS)
 
 
@@ -271,11 +272,17 @@ def tile_list_tenant_rank_scales_kernel(
 
         y_banks = {}
 
+        def base_first(h, n):
+            return (h, n) != (1, EARLY + 1)
+
+        def open_bank(h, n):
+            b = HALVES * n + h if n < EARLY else REUSE[h, n]
+            y_banks[h, n] = psum.tile([P, HALF], F32, name=f"y_bank{h}_{n}", tag=f"bank{b}")
+
         def base_pass(h, n, a):
             cols = slice(h * HALF, (h + 1) * HALF)
-            if a == 0:
-                b = HALVES * n + h if n < EARLY else REUSE[h, n]
-                y_banks[h, n] = psum.tile([P, HALF], F32, name=f"y_bank{h}_{n}", tag=f"bank{b}")
+            if a == 0 and base_first(h, n):
+                open_bank(h, n)
             if n < W4_FIRST:
                 codes = w4_early[a][:, 2 * n * P : 2 * (n + 1) * P]
             else:
@@ -286,20 +293,22 @@ def tile_list_tenant_rank_scales_kernel(
                 lhsT_scale=w4_planes[:, a, n * P : (n + 1) * P],
                 rhs=v_codes[a][:, cols].bitcast(FP8X4),
                 rhs_scale=v_scales[a][:, cols],
-                start=(a == 0),
-                stop=False,
+                start=(a == 0 and base_first(h, n)),
+                stop=(a == PASSES - 1 and not base_first(h, n)),
             )
 
         def close(h, n):
             c, m0 = divmod(n * P, WB_COLS)
+            if not base_first(h, n):
+                open_bank(h, n)
             nc.tensor.matmul_mx(
                 out=y_banks[h, n][:],
                 lhsT=wb_mx[c][0][:, m0 : m0 + P].bitcast(FP8X4),
                 lhsT_scale=wb_mx[c][1][:, m0 : m0 + P],
                 rhs=h_mx[h][0].bitcast(FP8X4),
                 rhs_scale=h_mx[h][1],
-                start=False,
-                stop=True,
+                start=(not base_first(h, n)),
+                stop=(base_first(h, n)),
             )
 
         def empty(h, n, result, on_vector):
@@ -332,16 +341,15 @@ def tile_list_tenant_rank_scales_kernel(
             scale_ranks(0, last, q * QUARTER, QUARTER)
         for q in range(2):
             weave_h(0, 1, q * QUARTER, QUARTER, nc.vector.tensor_copy)
-        for c in range(2):
-            weave_wb(c, nc.scalar.copy)
+        weave_wb(0, nc.scalar.copy)
+        weave_wb(1, nc.scalar.copy, 0, WB_SCALAR)
         for q in range(2):
             quantise_h(0, q)
         wb_mx = [quantise_wb(0)]
         scale_ranks(1, last, 0, QUARTER)
+        weave_wb(1, nc.vector.tensor_copy, WB_SCALAR, WB_COLS - WB_SCALAR)
         wb_mx.append(quantise_wb(1))
-        first_result = WB_AT + EARLY_COLS + WB_COLS
-        finish_half(0, 0, common[:, first_result : first_result + HALF], False)
-        for n in range(1, EARLY):
+        for n in range(EARLY):
             finish_half(0, n, new_result(0, n), False)
         for c0 in (QUARTER, QUARTER + P):
             scale_ranks(1, last, c0, P)
@@ -358,17 +366,22 @@ def tile_list_tenant_rank_scales_kernel(
         for n in range(EARLY, N_TILES):
             if n == EARLY + 1:
                 wb_mx.append(quantise_wb(3))
-            if n < N_TILES - 1:
-                for h in range(HALVES):
+            whole = keep.tile([P, S], F32, name=f"result{n}") if n < N_TILES - 1 else None
+            for h in range(HALVES):
+                if base_first(h, n) and whole is not None:
                     for a in range(PASSES):
                         base_pass(h, n, a)
-                result = keep.tile([P, S], F32, name=f"result{n}")
-                for h in range(HALVES):
-                    close(h, n)
-                    empty(h, n, result[:, h * HALF : (h + 1) * HALF], h == 0)
-                nc.sync.dma_start(out=out[n * P : (n + 1) * P, :], in_=result[:])
-            else:
-                for h in range(HALVES):
+            for h in range(HALVES):
+                if whole is None:
                     for a in range(PASSES):
                         base_pass(h, n, a)
-                    finish_half(h, n, new_result(h, n), h == 0)
+                close(h, n)
+                if not base_first(h, n):
+                    for a in range(PASSES):
+                        base_pass(h, n, a)
+                result = new_result(h, n) if whole is None else whole[:, h * HALF : (h + 1) * HALF]
+                empty(h, n, result, h == 0)
+                if whole is None:
+                    nc.sync.dma_start(out=out[n * P : (n + 1) * P, h * HALF : (h + 1) * HALF], in_=result)
+            if whole is not None:
+                nc.sync.dma_start(out=out[n * P : (n + 1) * P, :], in_=whole[:])

@@ -18,6 +18,7 @@ IDENTITY = mybir.ActivationFunctionType.Identity
 MULT = mybir.AluOpType.mult
 
 P = 128
+ROW_ALIGN = 256
 PACK = 4
 K_PASS = P * PACK
 PASSES = K // K_PASS
@@ -52,30 +53,30 @@ def tile_list_tenant_rank_scales_kernel(
         shared = ctx.enter_context(tc.tile_pool(name="shared", bufs=1))
         psum = ctx.enter_context(tc.psum_pool(name="psum", bufs=1))
 
-        offsets = keep.tile([P, S // LIST_ROWS], U16, name="offsets")
+        offsets = keep.tile([P, S // LIST_ROWS], U16, name="offsets", align_bytes=ROW_ALIGN)
 
-        tab_planes = shared.tile([P, T], U8, name="tab_planes", align_bytes=64, offset=0)
+        tab_planes = shared.tile([P, T], U8, name="tab_planes", align_bytes=ROW_ALIGN, offset=0)
         nc.gpsimd.memset(tab_planes[:].bitcast(I32), 0)
-        ba_row = keep.tile([P, R], F32, name="ba_row")
+        ba_row = keep.tile([P, R], F32, name="ba_row", align_bytes=ROW_ALIGN)
         nc.vector.memset(ba_row[:], 0.0)
-        bo_rows = keep.tile([P, P], F32, name="bo_rows")
+        bo_rows = keep.tile([P, P], F32, name="bo_rows", align_bytes=ROW_ALIGN)
         nc.vector.memset(bo_rows[:], 0.0)
         ident = keep.tile([P, P], F32, name="ident")
         make_identity(nc, ident[:])
-        v_planes = keep.tile([P, PASSES, S], U8, name="v_planes", align_bytes=64)
+        v_planes = keep.tile([P, PASSES, S], U8, name="v_planes", align_bytes=ROW_ALIGN)
         nc.vector.memset(v_planes[:].bitcast(I32), 0)
-        w4_planes = keep.tile([P, PASSES, N], U8, name="w4_planes", align_bytes=64)
+        w4_planes = keep.tile([P, PASSES, N], U8, name="w4_planes", align_bytes=ROW_ALIGN)
         nc.vector.memset(w4_planes[:].bitcast(I32), 0)
 
         def load_table(a):
-            win = keep.tile([P, T], U32, name=f"tab_win{a}", align_bytes=64)
+            win = keep.tile([P, T], U32, name=f"tab_win{a}", align_bytes=ROW_ALIGN)
             nc.sync.dma_start(
                 out=win[:].bitcast(I32),
                 in_=tab_words[a].rearrange("p t i -> p (t i)").bitcast(I32),
             )
             return win
 
-        wa_raw = [keep.tile([P, PACK, R], F32, name=f"wa_raw{a}") for a in range(PASSES)]
+        wa_raw = [keep.tile([P, PACK, R], F32, name=f"wa_raw{a}", align_bytes=ROW_ALIGN) for a in range(PASSES)]
 
         def load_wa(a, j0, j1):
             rows = wa[a * K_PASS : (a + 1) * K_PASS, :].rearrange("(p j) r -> p j r", j=PACK)
@@ -84,19 +85,19 @@ def tile_list_tenant_rank_scales_kernel(
         g_rows = gT.rearrange("(p t) c -> t p c", t=PACK)
 
         def load_g(t):
-            win = shared.tile([P, T], F32, name=f"g_win{t}", align_bytes=64, offset=G_AT + 4 * T * t)
+            win = shared.tile([P, T], F32, name=f"g_win{t}", align_bytes=ROW_ALIGN, offset=G_AT + 4 * T * t)
             nc.sync.dma_start(out=win[:], in_=g_rows[t])
             return win
 
         def load_w4_early(a):
-            codes = keep.tile([P, 2 * W4_FIRST * P], U8, name=f"w4_early{a}", align_bytes=64)
+            codes = keep.tile([P, 2 * W4_FIRST * P], U8, name=f"w4_early{a}", align_bytes=ROW_ALIGN)
             nc.sync.dma_start(out=codes[:].bitcast(I32), in_=w4_words[a][:, : 2 * W4_FIRST * P].bitcast(I32))
             return codes
 
         wb_rows = wb.rearrange("(p j) n -> p j n", j=PACK)
 
         def load_wb(name, c0, width):
-            flat = keep.tile([P, PACK * HALF], F32, name=name)
+            flat = keep.tile([P, PACK * HALF], F32, name=name, align_bytes=ROW_ALIGN)
             raw = flat[:].rearrange("p (j n) -> p j n", j=PACK)[:, :, :width]
             nc.sync.dma_start(out=raw, in_=wb_rows[:, :, c0 : c0 + width])
             return flat, raw
@@ -113,8 +114,8 @@ def tile_list_tenant_rank_scales_kernel(
         nc.sync.dma_start(out=bo_rows[0:N_TILES, :], in_=bo.rearrange("(c p) -> c p", p=P))
         load_wa(1, 0, PACK)
 
-        v_codes = [keep.tile([P, S], U32, name=f"v_codes{a}", align_bytes=64) for a in range(PASSES)]
-        picked = keep.tile([P, S], U8, name="picked", align_bytes=64)
+        v_codes = [keep.tile([P, S], U32, name=f"v_codes{a}", align_bytes=ROW_ALIGN) for a in range(PASSES)]
+        picked = keep.tile([P, S], U8, name="picked", align_bytes=ROW_ALIGN)
         nc.vector.tensor_copy(out=picked[:], in_=tab_planes[:].indirect(offsets[:]))
         for quad in (0, 2, 1, 3):
             p0 = quad * QUADRANT
@@ -133,12 +134,12 @@ def tile_list_tenant_rank_scales_kernel(
         w4_early = [load_w4_early(0)]
         g_win.append(load_g(PACK - 1))
         w4_early.append(load_w4_early(1))
-        common = keep.tile([P, WB_AT + PACK * EARLY_COLS], F32, name="common", align_bytes=64)
+        common = keep.tile([P, WB_AT + PACK * EARLY_COLS], F32, name="common", align_bytes=ROW_ALIGN)
         wb_early = common[:, WB_AT:].rearrange("p (j n) -> p j n", j=PACK)
         wb_raw0, wb_raw1 = wb_early[:, :, :WB_COLS], wb_early[:, :, WB_COLS:]
         nc.sync.dma_start(out=wb_raw0, in_=wb_rows[:, :, :WB_COLS])
         nc.sync.dma_start(out=wb_raw1, in_=wb_rows[:, :, WB_COLS : 2 * WB_COLS])
-        w4_late = keep.tile([P, PASSES, 2 * (N - W4_FIRST * P)], U8, name="w4_late", align_bytes=64)
+        w4_late = keep.tile([P, PASSES, 2 * (N - W4_FIRST * P)], U8, name="w4_late", align_bytes=ROW_ALIGN)
         nc.sync.dma_start(
             out=w4_late[:].bitcast(I32),
             in_=w4_words[:, :, 2 * W4_FIRST * P :].rearrange("a p c -> p a c").bitcast(I32),
@@ -154,18 +155,18 @@ def tile_list_tenant_rank_scales_kernel(
 
         wa_codes, wa_planes = [], []
         for a in range(PASSES):
-            woven = keep.tile([P, PACK * R], BF16, name=f"wa_woven{a}", align_bytes=64)
+            woven = keep.tile([P, PACK * R], BF16, name=f"wa_woven{a}", align_bytes=ROW_ALIGN)
             dst = woven[:].rearrange("p (t m j) -> p m j t", t=PACK, j=PACK)
             src = wa_raw[a][:].rearrange("p j (m t) -> p m j t", t=PACK)
             cut = WA_SCALAR[a]
             nc.scalar.copy(out=dst[:, :cut], in_=src[:, :cut])
             if cut < P:
                 nc.vector.tensor_copy(out=dst[:, cut:], in_=src[:, cut:])
-            codes = keep.tile([P, R], U32, name=f"wa_codes{a}", align_bytes=64)
+            codes = keep.tile([P, R], U32, name=f"wa_codes{a}", align_bytes=ROW_ALIGN)
             if a == 0:
-                plane = shared.tile([P, R], U8, name="wa_plane0", align_bytes=64, offset=0)
+                plane = shared.tile([P, R], U8, name="wa_plane0", align_bytes=ROW_ALIGN, offset=0)
             else:
-                plane = keep.tile([P, R], U8, name="wa_plane1", align_bytes=64)
+                plane = keep.tile([P, R], U8, name="wa_plane1", align_bytes=ROW_ALIGN)
             nc.vector.quantize_mx(out=codes[:].bitcast(FP8X4), scales=plane[:], in_=woven[:])
             wa_codes.append(codes)
             wa_planes.append(plane)
@@ -214,14 +215,14 @@ def tile_list_tenant_rank_scales_kernel(
                 first_product(*entry, 0)
 
         h4 = common[:, : PACK * S].rearrange("p (t c) -> p t c", t=PACK)
-        h_woven = [keep.tile([P, PACK * HALF], BF16, name=f"h_woven{h}", align_bytes=64)[:] for h in range(HALVES)]
+        h_woven = [keep.tile([P, PACK * HALF], BF16, name=f"h_woven{h}", align_bytes=ROW_ALIGN)[:] for h in range(HALVES)]
         wb_woven = {
-            c: keep.tile([P, PACK * WB_COLS], BF16, name=f"wb_woven{c}", align_bytes=64)[:] for c in range(N // WB_COLS)
+            c: keep.tile([P, PACK * WB_COLS], BF16, name=f"wb_woven{c}", align_bytes=ROW_ALIGN)[:] for c in range(N // WB_COLS)
         }
         h_mx = [
             (
-                keep.tile([P, HALF], U32, name=f"h_codes{h}", align_bytes=64)[:],
-                keep.tile([P, HALF], U8, name=f"h_plane{h}", align_bytes=64)[:],
+                keep.tile([P, HALF], U32, name=f"h_codes{h}", align_bytes=ROW_ALIGN)[:],
+                keep.tile([P, HALF], U8, name=f"h_plane{h}", align_bytes=ROW_ALIGN)[:],
             )
             for h in range(HALVES)
         ]
@@ -259,8 +260,8 @@ def tile_list_tenant_rank_scales_kernel(
             )
 
         def quantise_wb(c):
-            codes = keep.tile([P, WB_COLS], U32, name=f"wb_codes{c}", align_bytes=64)[:]
-            plane = keep.tile([P, WB_COLS], U8, name=f"wb_plane{c}", align_bytes=64)[:]
+            codes = keep.tile([P, WB_COLS], U32, name=f"wb_codes{c}", align_bytes=ROW_ALIGN)[:]
+            plane = keep.tile([P, WB_COLS], U8, name=f"wb_plane{c}", align_bytes=ROW_ALIGN)[:]
             width = P if c < 2 else WB_COLS
             for c0 in range(0, WB_COLS, width):
                 nc.vector.quantize_mx(
@@ -323,7 +324,7 @@ def tile_list_tenant_rank_scales_kernel(
             nc.sync.dma_start(out=out[n * P : (n + 1) * P, h * HALF : (h + 1) * HALF], in_=result)
 
         def new_result(h, n):
-            return keep.tile([P, HALF], F32, name=f"result{h}_{n}")[:]
+            return keep.tile([P, HALF], F32, name=f"result{h}_{n}", align_bytes=ROW_ALIGN)[:]
 
         for h, a in ((0, 0), (1, 0), (0, 1), (1, 1)):
             for n in range(EARLY):
@@ -366,7 +367,7 @@ def tile_list_tenant_rank_scales_kernel(
         for n in range(EARLY, N_TILES):
             if n == EARLY + 1:
                 wb_mx.append(quantise_wb(3))
-            whole = keep.tile([P, S], F32, name=f"result{n}") if n < N_TILES - 1 else None
+            whole = keep.tile([P, S], F32, name=f"result{n}", align_bytes=ROW_ALIGN) if n < N_TILES - 1 else None
             for h in range(HALVES):
                 if base_first(h, n) and whole is not None:
                     for a in range(PASSES):

@@ -60,7 +60,7 @@ def tile_list_tenant_rank_scales_kernel(
         ba_row = keep.tile([P, R], F32, name="ba_row", align_bytes=ROW_ALIGN)
         nc.vector.memset(ba_row[:], 0.0)
         bo_rows = keep.tile([P, P], F32, name="bo_rows", align_bytes=ROW_ALIGN)
-        nc.vector.memset(bo_rows[:], 0.0)
+        nc.scalar.copy(out=bo_rows[:], in_=ba_row[:, :P])
         ident = keep.tile([P, P], F32, name="ident")
         make_identity(nc, ident[:])
         v_planes = keep.tile([P, PASSES, S], U8, name="v_planes", align_bytes=ROW_ALIGN)
@@ -323,8 +323,11 @@ def tile_list_tenant_rank_scales_kernel(
             empty(h, n, result, on_vector)
             nc.sync.dma_start(out=out[n * P : (n + 1) * P, h * HALF : (h + 1) * HALF], in_=result)
 
+        results = {}
+
         def new_result(h, n):
-            return keep.tile([P, HALF], F32, name=f"result{h}_{n}", align_bytes=ROW_ALIGN)[:]
+            results[h, n] = keep.tile([P, HALF], F32, name=f"result{h}_{n}", align_bytes=ROW_ALIGN)[:]
+            return results[h, n]
 
         for h, a in ((0, 0), (1, 0), (0, 1), (1, 1)):
             for n in range(EARLY):

from contextlib import ExitStack

import concourse.mybir as mybir
from concourse.masks import make_identity

K, R, N, T, S = 1024, 512, 1024, 2048, 1024
FLOPS = 2 * S * (K * R + K * N + R * N)

F32 = mybir.dt.float32
BF16 = mybir.dt.bfloat16
I32 = mybir.dt.int32
U32 = mybir.dt.uint32
U16 = mybir.dt.uint16
U8 = mybir.dt.uint8
FP8X4 = mybir.dt.float8_e4m3fn_x4
FP4X4 = mybir.dt.float4_e2m1fn_x4
IDENTITY = mybir.ActivationFunctionType.Identity
MULT = mybir.AluOpType.mult

P = 128
ROW_ALIGN = 256
PACK = 4
K_PASS = P * PACK
PASSES = K // K_PASS
QUADRANT = 32
SCALE_ROWS = K_PASS // 32
LIST_ROWS = 16
LINE = 4
HALF = 512
HALVES = S // HALF
N_TILES = N // P
QUARTER = HALF // 2
WB_COLS = 256
EARLY = N_TILES // 2
EARLY_COLS = EARLY * P
W4_FIRST = EARLY
G_AT = T // 2
WB_SCALAR = 192
SPREAD = P // (PASSES * SCALE_ROWS)


WA_SCALAR = (80, 68)
WB_AT = PACK * S - HALF
REUSE = {(h, n): HALVES * ((2 * (n - EARLY) + h) % EARLY) + (2 * (n - EARLY) + h) // EARLY for n in range(EARLY, N_TILES) for h in range(HALVES)}


def tile_list_tenant_rank_scales_kernel(
    tc, tab_words, tab_scales, offs, wa, ba, gT, wb, w4_words, w4_scales, bo, out
):
    nc = tc.nc
    with ExitStack() as ctx:
        keep = ctx.enter_context(tc.tile_pool(name="keep", bufs=1))
        shared = ctx.enter_context(tc.tile_pool(name="shared", bufs=1))
        psum = ctx.enter_context(tc.psum_pool(name="psum", bufs=1))

        offsets = keep.tile([P, S // LIST_ROWS], U16, name="offsets", align_bytes=ROW_ALIGN)

        tab_planes = shared.tile([P, T], U8, name="tab_planes", align_bytes=ROW_ALIGN, offset=0)
        nc.gpsimd.memset(tab_planes[:].bitcast(I32), 0)
        ba_row = keep.tile([P, R], F32, name="ba_row", align_bytes=ROW_ALIGN)
        nc.vector.memset(ba_row[:], 0.0)
        bo_rows = keep.tile([P, P], F32, name="bo_rows", align_bytes=ROW_ALIGN)
        nc.scalar.copy(out=bo_rows[:], in_=ba_row[:, :P])
        ident = keep.tile([P, P], F32, name="ident")
        make_identity(nc, ident[:])
        v_planes = keep.tile([P, PASSES, S], U8, name="v_planes", align_bytes=ROW_ALIGN)
        nc.vector.memset(v_planes[:].bitcast(I32), 0)
        w4_planes = keep.tile([P, PASSES, N], U8, name="w4_planes", align_bytes=ROW_ALIGN)
        nc.vector.memset(w4_planes[:].bitcast(I32), 0)

        def load_table(a):
            win = keep.tile([P, T], U32, name=f"tab_win{a}", align_bytes=ROW_ALIGN)
            nc.sync.dma_start(
                out=win[:].bitcast(I32),
                in_=tab_words[a].rearrange("p t i -> p (t i)").bitcast(I32),
            )
            return win

        wa_raw = [keep.tile([P, PACK, R], F32, name=f"wa_raw{a}", align_bytes=ROW_ALIGN) for a in range(PASSES)]

        def load_wa(a, j0, j1):
            rows = wa[a * K_PASS : (a + 1) * K_PASS, :].rearrange("(p j) r -> p j r", j=PACK)
            nc.sync.dma_start(out=wa_raw[a][:, j0:j1, :], in_=rows[:, j0:j1, :])

        g_rows = gT.rearrange("(p t) c -> t p c", t=PACK)

        def load_g(t):
            win = shared.tile([P, T], F32, name=f"g_win{t}", align_bytes=ROW_ALIGN, offset=G_AT + 4 * T * t)
            nc.sync.dma_start(out=win[:], in_=g_rows[t])
            return win

        def load_w4_early(a):
            codes = keep.tile([P, 2 * W4_FIRST * P], U8, name=f"w4_early{a}", align_bytes=ROW_ALIGN)
            nc.sync.dma_start(out=codes[:].bitcast(I32), in_=w4_words[a][:, : 2 * W4_FIRST * P].bitcast(I32))
            return codes

        wb_rows = wb.rearrange("(p j) n -> p j n", j=PACK)

        def load_wb(name, c0, width):
            flat = keep.tile([P, PACK * HALF], F32, name=name, align_bytes=ROW_ALIGN)
            raw = flat[:].rearrange("p (j n) -> p j n", j=PACK)[:, :, :width]
            nc.sync.dma_start(out=raw, in_=wb_rows[:, :, c0 : c0 + width])
            return flat, raw

        load_wa(0, 0, 2)
        nc.sync.dma_start(offsets[:], offs)
        nc.sync.dma_start(
            out=tab_planes[0:P:SPREAD, :].bitcast(I32),
            in_=tab_scales.rearrange("a q c -> q a c").bitcast(I32),
        )
        load_wa(0, 2, PACK)
        tab_win = [load_table(0)]
        nc.sync.dma_start(out=ba_row[0:1, :], in_=ba.rearrange("(o r) -> o r", o=1))
        nc.sync.dma_start(out=bo_rows[0:N_TILES, :], in_=bo.rearrange("(c p) -> c p", p=P))
        load_wa(1, 0, PACK)

        v_codes = [keep.tile([P, S], U32, name=f"v_codes{a}", align_bytes=ROW_ALIGN) for a in range(PASSES)]
        picked = keep.tile([P, S], U8, name="picked", align_bytes=ROW_ALIGN)
        nc.vector.tensor_copy(out=picked[:], in_=tab_planes[:].indirect(offsets[:]))
        for quad in (0, 2, 1, 3):
            p0 = quad * QUADRANT
            nc.sync.dma_start(
                out=v_planes[p0 : p0 + 4, :, :].bitcast(I32),
                in_=picked[p0 : p0 + QUADRANT : SPREAD, :].bitcast(I32),
            )
        tab_win.append(load_table(1))
        v_scales = [v_planes[:, a, :] for a in range(PASSES)]
        g_win = [load_g(t) for t in range(PACK - 1)]
        for r in range(4):
            nc.sync.dma_start(
                out=w4_planes[r:P:QUADRANT, :, :].bitcast(I32),
                in_=w4_scales[:, r:SCALE_ROWS:4, :].rearrange("a q c -> q a c").bitcast(I32),
            )
        w4_early = [load_w4_early(0)]
        g_win.append(load_g(PACK - 1))
        w4_early.append(load_w4_early(1))
        common = keep.tile([P, WB_AT + PACK * EARLY_COLS], F32, name="common", align_bytes=ROW_ALIGN)
        wb_early = common[:, WB_AT:].rearrange("p (j n) -> p j n", j=PACK)
        wb_raw0, wb_raw1 = wb_early[:, :, :WB_COLS], wb_early[:, :, WB_COLS:]
        nc.sync.dma_start(out=wb_raw0, in_=wb_rows[:, :, :WB_COLS])
        nc.sync.dma_start(out=wb_raw1, in_=wb_rows[:, :, WB_COLS : 2 * WB_COLS])
        w4_late = keep.tile([P, PASSES, 2 * (N - W4_FIRST * P)], U8, name="w4_late", align_bytes=ROW_ALIGN)
        nc.sync.dma_start(
            out=w4_late[:].bitcast(I32),
            in_=w4_words[:, :, 2 * W4_FIRST * P :].rearrange("a p c -> p a c").bitcast(I32),
        )
        wb_late = load_wb("wb_late", EARLY_COLS, N - EARLY_COLS)[1]
        wb_raw = [wb_raw0, wb_raw1, wb_late[:, :, :WB_COLS], wb_late[:, :, WB_COLS:]]

        ba_bank = psum.tile([P, PACK, P], F32, name="ba_bank", tag=f"bank{N_TILES - 2}")
        for t in range(PACK):
            nc.tensor.transpose(ba_bank[:, t, :], ba_row[:, t:R:PACK], ident[:])
        ba_cols = keep.tile([P, PACK], F32, name="ba_cols")
        nc.scalar.activation(out=ba_cols[:], in_=ba_bank[:, :, 0], func=IDENTITY)

        wa_codes, wa_planes = [], []
        for a in range(PASSES):
            woven = keep.tile([P, PACK * R], BF16, name=f"wa_woven{a}", align_bytes=ROW_ALIGN)
            dst = woven[:].rearrange("p (t m j) -> p m j t", t=PACK, j=PACK)
            src = wa_raw[a][:].rearrange("p j (m t) -> p m j t", t=PACK)
            cut = WA_SCALAR[a]
            nc.scalar.copy(out=dst[:, :cut], in_=src[:, :cut])
            if cut < P:
                nc.vector.tensor_copy(out=dst[:, cut:], in_=src[:, cut:])
            codes = keep.tile([P, R], U32, name=f"wa_codes{a}", align_bytes=ROW_ALIGN)
            if a == 0:
                plane = shared.tile([P, R], U8, name="wa_plane0", align_bytes=ROW_ALIGN, offset=0)
            else:
                plane = keep.tile([P, R], U8, name="wa_plane1", align_bytes=ROW_ALIGN)
            nc.vector.quantize_mx(out=codes[:].bitcast(FP8X4), scales=plane[:], in_=woven[:])
            wa_codes.append(codes)
            wa_planes.append(plane)

        bo_bank = psum.tile([P, P], F32, name="bo_bank", tag=f"bank{N_TILES - 1}")
        nc.tensor.transpose(bo_bank[:], bo_rows[:], ident[:])
        bo_cols = keep.tile([P, N_TILES], F32, name="bo_cols")
        nc.scalar.activation(out=bo_cols[:], in_=bo_bank[:, 0:N_TILES], func=IDENTITY)

        def part_list(c0, width):
            return offsets[:, c0 // LIST_ROWS : (c0 + width) // LIST_ROWS]

        for a, cuts in enumerate(((0, S), range(0, S + 1, QUARTER))):
            for c0, c1 in zip(cuts, cuts[1:]):
                nc.vector.tensor_copy(out=v_codes[a][:, c0:c1], in_=tab_win[a][:].indirect(part_list(c0, c1 - c0)))

        a_sb = [keep.tile([P, S], F32, name=f"a_sb{t}") for t in range(PACK)]
        sums = [(h, 0, q * QUARTER, QUARTER, N_TILES - 1 - h if q else h) for h in range(HALVES) for q in range(2)]
        sums.extend((h, t, 0, HALF, HALVES * t + h) for t in range(1, PACK) for h in range(HALVES))
        a_banks = {}

        def first_product(h, t, c0, width, b, a):
            cols = slice(h * HALF + c0, h * HALF + c0 + width)
            opens = (h, t, c0) not in a_banks
            if opens:
                a_banks[h, t, c0] = psum.tile([P, HALF], F32, name=f"a_bank{h}_{t}_{c0}", tag=f"bank{b}")
            bank = a_banks[h, t, c0][:, :width]
            nc.tensor.matmul_mx(
                out=bank,
                lhsT=wa_codes[a][:, t * P : (t + 1) * P].bitcast(FP8X4),
                lhsT_scale=wa_planes[a][:, t * P : (t + 1) * P],
                rhs=v_codes[a][:, cols].bitcast(FP8X4),
                rhs_scale=v_scales[a][:, cols],
                start=opens,
                stop=not opens,
            )
            if not opens:
                nc.scalar.activation(out=a_sb[t][:, cols], in_=bank, func=IDENTITY, bias=ba_cols[:, t : t + 1])

        opened_early = sums[:7]
        for entry in opened_early:
            first_product(*entry, 0)
        for entry in sums:
            first_product(*entry, 1)
            if entry not in opened_early:
                first_product(*entry, 0)

        h4 = common[:, : PACK * S].rearrange("p (t c) -> p t c", t=PACK)
        h_woven = [keep.tile([P, PACK * HALF], BF16, name=f"h_woven{h}", align_bytes=ROW_ALIGN)[:] for h in range(HALVES)]
        wb_woven = {
            c: keep.tile([P, PACK * WB_COLS], BF16, name=f"wb_woven{c}", align_bytes=ROW_ALIGN)[:] for c in range(N // WB_COLS)
        }
        h_mx = [
            (
                keep.tile([P, HALF], U32, name=f"h_codes{h}", align_bytes=ROW_ALIGN)[:],
                keep.tile([P, HALF], U8, name=f"h_plane{h}", align_bytes=ROW_ALIGN)[:],
            )
            for h in range(HALVES)
        ]

        def scale_ranks(h, t, c0, width):
            nc.vector.tensor_tensor(
                out=h4[:, t, h * HALF + c0 : h * HALF + c0 + width],
                in0=g_win[t][:].indirect(part_list(h * HALF + c0, width)),
                in1=a_sb[t][:, h * HALF + c0 : h * HALF + c0 + width],
                op=MULT,
            )

        def weave_h(h, u, c0, width, weave):
            weave(
                out=h_woven[h][:, PACK * c0 : PACK * (c0 + width)].rearrange(
                    "p (c i u e) -> p u c e i", i=LINE, u=2, e=2
                )[:, u],
                in_=h4[:, 2 * u : 2 * u + 2, h * HALF + c0 : h * HALF + c0 + width].rearrange(
                    "p e (c i) -> p c e i", i=LINE
                ),
            )

        def quantise_h(h, q):
            cols = slice(q * QUARTER, (q + 1) * QUARTER)
            nc.vector.quantize_mx(
                out=h_mx[h][0][:, cols].bitcast(FP8X4),
                scales=h_mx[h][1][:, cols],
                in_=h_woven[h][:, PACK * q * QUARTER : PACK * (q + 1) * QUARTER],
            )

        def weave_wb(c, weave, c0=0, width=WB_COLS):
            weave(
                out=wb_woven[c][:, PACK * c0 : PACK * (c0 + width)].rearrange("p (c i j) -> p c j i", i=LINE, j=PACK),
                in_=wb_raw[c][:, :, c0 : c0 + width].rearrange("p j (c i) -> p c j i", i=LINE),
            )

        def quantise_wb(c):
            codes = keep.tile([P, WB_COLS], U32, name=f"wb_codes{c}", align_bytes=ROW_ALIGN)[:]
            plane = keep.tile([P, WB_COLS], U8, name=f"wb_plane{c}", align_bytes=ROW_ALIGN)[:]
            width = P if c < 2 else WB_COLS
            for c0 in range(0, WB_COLS, width):
                nc.vector.quantize_mx(
                    out=codes[:, c0 : c0 + width].bitcast(FP8X4),
                    scales=plane[:, c0 : c0 + width],
                    in_=wb_woven[c][:, PACK * c0 : PACK * (c0 + width)],
                )
            return codes, plane

        y_banks = {}

        def base_first(h, n):
            return (h, n) != (1, EARLY + 1)

        def open_bank(h, n):
            b = HALVES * n + h if n < EARLY else REUSE[h, n]
            y_banks[h, n] = psum.tile([P, HALF], F32, name=f"y_bank{h}_{n}", tag=f"bank{b}")

        def base_pass(h, n, a):
            cols = slice(h * HALF, (h + 1) * HALF)
            if a == 0 and base_first(h, n):
                open_bank(h, n)
            if n < W4_FIRST:
                codes = w4_early[a][:, 2 * n * P : 2 * (n + 1) * P]
            else:
                codes = w4_late[:, a, 2 * (n - W4_FIRST) * P : 2 * (n - W4_FIRST + 1) * P]
            nc.tensor.matmul_mx(
                out=y_banks[h, n][:],
                lhsT=codes.bitcast(FP4X4),
                lhsT_scale=w4_planes[:, a, n * P : (n + 1) * P],
                rhs=v_codes[a][:, cols].bitcast(FP8X4),
                rhs_scale=v_scales[a][:, cols],
                start=(a == 0 and base_first(h, n)),
                stop=(a == PASSES - 1 and not base_first(h, n)),
            )

        def close(h, n):
            c, m0 = divmod(n * P, WB_COLS)
            if not base_first(h, n):
                open_bank(h, n)
            nc.tensor.matmul_mx(
                out=y_banks[h, n][:],
                lhsT=wb_mx[c][0][:, m0 : m0 + P].bitcast(FP8X4),
                lhsT_scale=wb_mx[c][1][:, m0 : m0 + P],
                rhs=h_mx[h][0].bitcast(FP8X4),
                rhs_scale=h_mx[h][1],
                start=(not base_first(h, n)),
                stop=(base_first(h, n)),
            )

        def empty(h, n, result, on_vector):
            if on_vector:
                nc.vector.tensor_scalar_add(out=result, in0=y_banks[h, n][:], scalar1=bo_cols[:, n : n + 1])
            else:
                nc.scalar.activation(out=result, in_=y_banks[h, n][:], func=IDENTITY, bias=bo_cols[:, n : n + 1])

        def finish_half(h, n, result, on_vector):
            close(h, n)
            empty(h, n, result, on_vector)
            nc.sync.dma_start(out=out[n * P : (n + 1) * P, h * HALF : (h + 1) * HALF], in_=result)

        results = {}

        def new_result(h, n):
            results[h, n] = keep.tile([P, HALF], F32, name=f"result{h}_{n}", align_bytes=ROW_ALIGN)[:]
            return results[h, n]

        for h, a in ((0, 0), (1, 0), (0, 1), (1, 1)):
            for n in range(EARLY):
                base_pass(h, n, a)

        for q in range(2):
            scale_ranks(0, 0, q * QUARTER, QUARTER)
        scale_ranks(1, 0, 0, HALF)
        for h in range(HALVES):
            scale_ranks(h, 1, 0, HALF)
            weave_h(h, 0, 0, HALF, nc.scalar.copy)
        scale_ranks(0, 2, 0, S)
        last = PACK - 1
        for q in range(2):
            scale_ranks(0, last, q * QUARTER, QUARTER)
        for q in range(2):
            weave_h(0, 1, q * QUARTER, QUARTER, nc.vector.tensor_copy)
        weave_wb(0, nc.scalar.copy)
        weave_wb(1, nc.scalar.copy, 0, WB_SCALAR)
        for q in range(2):
            quantise_h(0, q)
        wb_mx = [quantise_wb(0)]
        scale_ranks(1, last, 0, QUARTER)
        weave_wb(1, nc.vector.tensor_copy, WB_SCALAR, WB_COLS - WB_SCALAR)
        wb_mx.append(quantise_wb(1))
        for n in range(EARLY):
            finish_half(0, n, new_result(0, n), False)
        for c0 in (QUARTER, QUARTER + P):
            scale_ranks(1, last, c0, P)
        weave_h(1, 1, 0, HALF - P, nc.vector.tensor_copy)
        weave_h(1, 1, HALF - P, P, nc.vector.tensor_copy)
        for q in range(2):
            quantise_h(1, q)
        weave_wb(2, nc.vector.tensor_copy)
        weave_wb(3, nc.vector.tensor_copy, 0, P)
        wb_mx.append(quantise_wb(2))
        weave_wb(3, nc.vector.tensor_copy, P, P)
        for n in range(EARLY):
            finish_half(1, n, new_result(1, n), n == EARLY - 1)
        for n in range(EARLY, N_TILES):
            if n == EARLY + 1:
                wb_mx.append(quantise_wb(3))
            whole = keep.tile([P, S], F32, name=f"result{n}", align_bytes=ROW_ALIGN) if n < N_TILES - 1 else None
            for h in range(HALVES):
                if base_first(h, n) and whole is not None:
                    for a in range(PASSES):
                        base_pass(h, n, a)
            for h in range(HALVES):
                if whole is None:
                    for a in range(PASSES):
                        base_pass(h, n, a)
                close(h, n)
                if not base_first(h, n):
                    for a in range(PASSES):
                        base_pass(h, n, a)
                result = new_result(h, n) if whole is None else whole[:, h * HALF : (h + 1) * HALF]
                empty(h, n, result, h == 0)
                if whole is None:
                    nc.sync.dma_start(out=out[n * P : (n + 1) * P, h * HALF : (h + 1) * HALF], in_=result)
            if whole is not None:
                nc.sync.dma_start(out=out[n * P : (n + 1) * P, :], in_=whole[:])
